import numpy as np
import ml_dtypes


def mxq(x, axis, fmt="e4m3"):
    dtype, down = {"e4m3": (ml_dtypes.float8_e4m3fn, 7), "e5m2": (ml_dtypes.float8_e5m2, 14)}[fmt]
    v = np.moveaxis(np.asarray(x, np.float32).astype(ml_dtypes.bfloat16).astype(np.float64), axis, -1)
    blocks = v.reshape(v.shape[:-1] + (-1, 32))
    amax = np.abs(blocks).max(-1, keepdims=True)
    byte = np.maximum(np.where(amax > 0, np.frexp(amax)[1] - 1 + 127, 0) - down, 1)
    scale = np.exp2(byte - 127.0)
    codes = (blocks / scale).astype(np.float32).astype(dtype).astype(np.float64)
    return np.moveaxis((codes * scale).reshape(v.shape), -1, axis)


WIDE = False


def mx_kscale(k):
    if not WIDE:
        return np.ones(k)
    levels = np.array([10, -10, 5, -5, 0])
    if k % 512:
        return np.exp2(np.random.permutation(np.resize(levels, k // 32))).repeat(32)
    a = np.empty((k // 512, 16))
    for p in range(k // 512):
        a[p, :8] = np.random.permutation(np.resize(levels, 8))
        for g in range(8):
            far = levels[np.abs(levels - a[p, g]) >= 10]
            a[p, g + 8] = far[np.random.randint(len(far))]
    return np.exp2(a.ravel()).repeat(32)


def f64(x):
    return np.asarray(x).astype(np.float64)


def striped(idx):
    return np.tile(idx.reshape(-1, 16).T, (8, 1)).astype(np.uint16)


def unstriped(offs):
    return offs[:16].T.reshape(-1).astype(np.int64)


E2M1 = np.array([0.0, 0.5, 1.0, 1.5, 2.0, 3.0, 4.0, 6.0, -0.0, -0.5, -1.0, -1.5, -2.0, -3.0, -4.0, -6.0])


def pack_weight(w, fmt):
    k, n = w.shape
    w = f64(np.asarray(w, np.float32).astype(ml_dtypes.bfloat16)).reshape(k // 32, 32, n)
    amax = np.abs(w).max(1)
    if fmt == "e4m3":
        byte = np.frexp(amax)[1] - 1 + 127 - 7
    else:
        mant, ex = np.frexp(amax / 6.0)
        byte = np.where(mant > 0.5, ex, ex - 1) + 127
    byte = np.clip(np.where(amax > 0, byte, 1), 1, 254)
    scaled = (w * np.exp2(127.0 - byte)[:, None, :]).reshape(k, n).astype(np.float32)
    by_word = np.ascontiguousarray(scaled.reshape(k // 512, 128, 4, n).transpose(0, 1, 3, 2))
    if fmt == "e4m3":
        words = by_word.astype(ml_dtypes.float8_e4m3fn).view(np.uint8)
    else:
        c = by_word.astype(ml_dtypes.float4_e2m1fn).view(np.uint8) & 0xF
        words = (c[..., 0::2] | (c[..., 1::2] << 4)).reshape(k // 512, 128, 2 * n)
    return np.ascontiguousarray(words), np.ascontiguousarray(byte.astype(np.uint8).reshape(k // 512, 16, n))


def unpack_weight(words, scales, fmt):
    g, _, n = scales.shape
    words = np.ascontiguousarray(words).reshape(g, 128, n, -1)
    if fmt == "e4m3":
        vals = words.view(ml_dtypes.float8_e4m3fn).astype(np.float64)
    else:
        nib = np.empty((g, 128, n, 4), np.uint8)
        nib[..., 0::2] = words & 0xF
        nib[..., 1::2] = words >> 4
        vals = E2M1[nib]
    vals = vals * np.repeat(np.exp2(scales.astype(np.float64) - 127.0), 8, axis=1)[..., None]
    return vals.transpose(0, 1, 3, 2).reshape(g * 512, n)


def planes(y):
    n, m = y.shape
    v = y.astype(np.float32).astype(ml_dtypes.bfloat16).astype(np.float64).reshape(n // 32, 32, m)
    top = np.abs(v).max(1)
    byte = np.clip(np.where(top > 0, np.frexp(top)[1] - 1 + 127 - 7, 1), 1, 254)
    codes = (v * np.exp2(127.0 - byte)[:, None, :]).reshape(n, m).astype(np.float32).astype(ml_dtypes.float8_e4m3fn).view(np.uint8)
    words = codes.reshape(n // 512, 128, 4, m).transpose(0, 1, 3, 2)
    return np.ascontiguousarray(words), np.ascontiguousarray(byte.astype(np.uint8).reshape(n // 512, 16, m))


def gelu(v):
    return 0.5 * v * (1.0 + np.tanh(np.sqrt(2.0 / np.pi) * (v + 0.044715 * v**3)))


K, T, E, C = 512, 512, 4, 256


def deal():
    first = np.random.permutation(np.repeat(np.arange(E), T // E))
    second = (first + 1 + np.random.permutation(np.repeat(np.arange(E - 1), -(-T // (E - 1)))[:T])) % E
    while np.bincount(second, minlength=E).max() != T // E:
        load = np.bincount(second, minlength=E); hi, lo = int(load.argmax()), int(load.argmin())
        t = np.flatnonzero((second == hi) & (first != lo))[0]; second[t] = lo
    slot_token = np.empty(E * C, np.int64); pos = np.empty((2, T), np.int64); fill = np.zeros(E, np.int64)
    place = np.stack([np.random.permutation(C) for _ in range(E)])
    for r, deal in enumerate((first, second)):
        for t in np.random.permutation(T):
            e = deal[t]; j = e * C + place[e, fill[e]]; fill[e] += 1; slot_token[j] = t; pos[r, t] = j
    g = np.random.uniform(0.2, 0.8, T)
    return slot_token, pos, np.stack([g, 1.0 - g])


def by_expert(wq, xq):
    return np.concatenate([wq[e].T @ xq[:, e * C:(e + 1) * C] for e in range(E)], axis=1)


def setup_inputs():
    n = np.random.standard_normal
    s = mx_kscale(K)
    slots1, pos1, g1 = deal()
    slots2, pos2, g2 = deal()
    x = pack_weight(n((K, T)) * s[:, None], "e4m3")
    w = [pack_weight(m, "e2m1") for m in n((E, K, K)) / np.sqrt(K) / s[None, :, None] * s]
    return {
        "x_words": x[0],
        "x_scales": x[1],
        "w_words": np.stack([m[0] for m in w]),
        "w_scales": np.stack([m[1] for m in w]),
        "gate1": (np.stack([np.tile(r, (128, 1)) for r in g1])).astype(np.float32),
        "gate2": (np.stack([np.tile(r, (128, 1)) for r in g2])).astype(np.float32),
        "offs": striped(slots1),
        "pos1": striped(pos1[0]),
        "pos2": striped(pos1[1]),
        "offs2": striped(slots2),
        "pos3": striped(pos2[0]),
        "pos4": striped(pos2[1]),
    }


def reference(x_words, x_scales, w_words, w_scales, gate1, gate2, offs, pos1, pos2, offs2, pos3, pos4):
    w = np.stack([unpack_weight(w_words[e], w_scales[e], "e2m1") for e in range(E)])
    idx, idx2 = unstriped(offs), unstriped(offs2)
    y = gelu(by_expert(w, unpack_weight(x_words, x_scales, "e4m3")[:, idx]))
    c = sum(f64(gate1[r, :1]) * y[:, unstriped(p)] for r, p in enumerate((pos1, pos2)))
    z = gelu(by_expert(w, mxq(c[:, idx2], 0, "e4m3")))
    out = sum(f64(gate2[r, :1]) * z[:, unstriped(p)] for r, p in enumerate((pos3, pos4)))
    out_0 = out
    return (out_0,) + planes(out_0)

@@ -1,0 +1,178 @@
+from contextlib import ExitStack
+
+import concourse.mybir as mybir
+
+K, T, E, C = 512, 512, 4, 256
+S = E * C
+P = 128
+PACK = 4
+FLOPS = 2 * 2 * K * K * S
+
+F32 = mybir.dt.float32
+BF16 = mybir.dt.bfloat16
+I32 = mybir.dt.int32
+U32 = mybir.dt.uint32
+U16 = mybir.dt.uint16
+U8 = mybir.dt.uint8
+FP8X4 = mybir.dt.float8_e4m3fn_x4
+FP4X4 = mybir.dt.float4_e2m1fn_x4
+MULT = mybir.AluOpType.mult
+ADD = mybir.AluOpType.add
+GELU = mybir.ActivationFunctionType.Gelu_apprx_tanh
+COPY = mybir.ActivationFunctionType.Copy
+COLS = C // 16
+
+
+def tile_moe_uni_gelu_kernel(
+    tc, x_words, x_scales, w_words, w_scales, gate1, gate2, offs, pos1, pos2, offs2, pos3, pos4, out_0, out_1, out_2
+):
+    nc = tc.nc
+    with ExitStack() as ctx:
+        lists = ctx.enter_context(tc.tile_pool(name="lists", bufs=1))
+        keep = ctx.enter_context(tc.tile_pool(name="keep", bufs=1))
+        psum = ctx.enter_context(tc.psum_pool(name="psum", bufs=1))
+
+        def load_list(name, src):
+            tile = lists.tile(list(src.shape), U16, name=name)
+            nc.sync.dma_start(tile[:], src)
+            return tile
+
+        xs = keep.tile([P, T], U8, name="xs", align_bytes=64)
+        ws = keep.tile([P, E * K], U8, name="ws", align_bytes=64)
+        nc.gpsimd.memset(xs[:].bitcast(I32), 0)
+        nc.vector.memset(ws[:].bitcast(I32), 0)
+
+        offs_t = load_list("offs_t", offs)
+        xw = keep.tile([P, T], I32, name="xw", tag="early", align_bytes=64)
+        nc.sync.dma_start(xw[:], x_words[0].rearrange("p t d -> p (t d)").bitcast(I32))
+        xs_rows = x_scales[0].bitcast(I32).rearrange("(q r) n -> r q n", r=4)
+        for r in range(4):
+            nc.sync.dma_start(xs[r:P:32, :].bitcast(I32), xs_rows[r])
+        ww = keep.tile([P, E * 2 * K], U8, name="ww", tag="late", align_bytes=64)
+        nc.sync.dma_start(
+            ww[:].bitcast(I32).rearrange("p (e n) -> p e n", e=E),
+            w_words.rearrange("e s p n -> p (e s) n").bitcast(I32),
+        )
+        ws_rows = w_scales.bitcast(I32).rearrange("e s (q r) n -> r q (e s) n", r=4)
+        for r in range(4):
+            nc.sync.dma_start(ws[r:P:32, :].bitcast(I32).rearrange("q (e n) -> q e n", e=E), ws_rows[r])
+        pos1_t = load_list("pos1_t", pos1)
+        pos2_t = load_list("pos2_t", pos2)
+        offs2_t = load_list("offs2_t", offs2)
+        pos3_t = load_list("pos3_t", pos3)
+        pos4_t = load_list("pos4_t", pos4)
+
+        wwp = [keep.tile([P, E * 2 * P], U8, name=f"wwp{t}", align_bytes=64) for t in range(PACK)]
+        wsp = [keep.tile([P, E * P], U8, name=f"wsp{t}", align_bytes=64) for t in range(PACK)]
+
+        def deal_weights(t):
+            nc.vector.tensor_copy(wwp[t][:].bitcast(U16), ww[:].bitcast(U16).rearrange("p (m t) -> p m t", t=PACK)[:, :, t])
+            nc.vector.tensor_copy(wsp[t][:], ws[:].rearrange("p (m t) -> p m t", t=PACK)[:, :, t])
+
+        def expert_plane(banks, y, words, scales, e, t):
+            acc = banks[t][e // 2][:, (e % 2) * C : (e % 2 + 1) * C]
+            nc.tensor.matmul_mx(
+                out=acc,
+                lhsT=wwp[t][:, e * 2 * P : (e + 1) * 2 * P].bitcast(FP4X4),
+                lhsT_scale=wsp[t][:, e * P : (e + 1) * P],
+                rhs=words[:].bitcast(FP8X4),
+                rhs_scale=scales[:],
+                start=True,
+                stop=True,
+            )
+            nc.scalar.activation(y[t][:, e * C : (e + 1) * C], acc, GELU)
+
+        banks = [[psum.tile([P, 2 * C], F32, name=f"bank{t}_{h}") for h in range(2)] for t in range(PACK)]
+
+        gw = [keep.tile([P, C], U32, name=f"gw{e}", align_bytes=64) for e in range(E)]
+        gs = [keep.tile([P, C], U8, name=f"gs{e}", align_bytes=64) for e in range(E)]
+        y = [keep.tile([P, S], F32, name=f"y{t}") for t in range(PACK)]
+        for e in range(E):
+            nc.vector.tensor_copy(gw[e][:], xw[:].bitcast(U32).indirect(offs_t[:, e * COLS : (e + 1) * COLS]))
+        g1 = keep.tile([P, 2, T], F32, name="g1", tag="early", align_bytes=64)
+        nc.sync.dma_start(g1[:], gate1.rearrange("r p t -> p r t"))
+        for e in range(E):
+            nc.vector.tensor_copy(gs[e][:], xs[:].indirect(offs_t[:, e * COLS : (e + 1) * COLS]))
+            if e < 2:
+                deal_weights(e)
+        deal_weights(2)
+        deal_weights(3)
+        g2 = keep.tile([P, 2, T], F32, name="g2", tag="late", align_bytes=64)
+        nc.sync.dma_start(g2[:], gate2.rearrange("r p t -> p r t"))
+        for t in range(PACK):
+            for e in range(E):
+                expert_plane(banks, y, gw[e], gs[e], e, t)
+
+        a = keep.tile([P, PACK, T], F32, name="a")
+        b = keep.tile([P, PACK, T], F32, name="b")
+        c_single = [keep.tile([P, T], BF16, name=f"c{t}", align_bytes=64) for t in range(2)]
+        c_pair = keep.tile([P, T, 2], BF16, name="c_pair", align_bytes=64)
+        xq = [keep.tile([P, C, PACK], BF16, name=f"xq{e}", align_bytes=64) for e in range(E)]
+
+        def first(dst, src, pos, gate, t):
+            nc.vector.tensor_tensor(dst[:, t, :], src[t][:].indirect(pos[:]), gate, MULT)
+
+        def gather_single(t):
+            nc.vector.tensor_tensor(c_single[t][:], a[:, t, :], b[:, t, :], ADD)
+            for e in range(E):
+                nc.scalar.activation(xq[e][:, :, t], c_single[t][:].indirect(offs2_t[:, e * COLS : (e + 1) * COLS]), COPY)
+
+        for t in range(PACK):
+            first(a, y, pos1_t, g1[:, 0, :], t)
+            if t in (1, 2):
+                gather_single(t - 1)
+            first(b, y, pos2_t, g1[:, 1, :], t)
+        nc.vector.tensor_tensor(
+            c_pair[:], a[:, 2:4, :].rearrange("p u t -> p t u"), b[:, 2:4, :].rearrange("p u t -> p t u"), ADD
+        )
+
+        qw = [keep.tile([P, C], U32, name=f"qw{e}", align_bytes=64) for e in range(E)]
+        qs = [keep.tile([P, C], U8, name=f"qs{e}", align_bytes=64) for e in range(E)]
+        z = [keep.tile([P, S], F32, name=f"z{t}") for t in range(PACK)]
+        c_words = c_pair[:].rearrange("p t u -> p (t u)").bitcast(U32)
+
+        def quantise(e):
+            nc.vector.quantize_mx(out=qw[e][:].bitcast(FP8X4), scales=qs[e][:], in_=xq[e][:].rearrange("p c t -> p (c t)"))
+
+        for e in range(E):
+            dst = xq[e][:].rearrange("p c t -> p (c t)").bitcast(U32).rearrange("p (c u) -> p c u", u=2)[:, :, 1]
+            nc.vector.tensor_copy(dst, c_words.indirect(offs2_t[:, e * COLS : (e + 1) * COLS]))
+            if e > 0:
+                quantise(e - 1)
+        quantise(E - 1)
+        for e in range(E - 1):
+            for t in range(PACK - 1):
+                expert_plane(banks, z, qw[e], qs[e], e, t)
+        for t in range(PACK - 1):
+            expert_plane(banks, z, qw[E - 1], qs[E - 1], E - 1, t)
+        for e in range(E):
+            expert_plane(banks, z, qw[e], qs[e], e, PACK - 1)
+
+        a2 = keep.tile([P, PACK, T], F32, name="a2")
+        b2 = keep.tile([P, PACK, T], F32, name="b2")
+        o = [keep.tile([P, 2, T], F32, name=f"o{u}") for u in range(2)]
+        oq = keep.tile([P, T, PACK], BF16, name="oq", align_bytes=64)
+        out_rows = out_0.rearrange("(p t) n -> p t n", t=PACK)
+
+        def finish(t):
+            nc.vector.tensor_tensor(o[t // 2][:, t % 2, :], a2[:, t, :], b2[:, t, :], ADD)
+            nc.sync.dma_start(out_rows[:, t, :], o[t // 2][:, t % 2, :])
+
+        for t in range(PACK):
+            first(a2, z, pos3_t, g2[:, 0, :], t)
+            if t > 0:
+                finish(t - 1)
+            if t == 2:
+                nc.scalar.copy(oq[:, :, 0:2], o[0][:].rearrange("p u t -> p t u"))
+            first(b2, z, pos4_t, g2[:, 1, :], t)
+        finish(PACK - 1)
+        nc.vector.tensor_copy(oq[:, :, 2:4], o[1][:].rearrange("p u t -> p t u"))
+
+        ow = keep.tile([P, T], I32, name="ow", align_bytes=64)
+        osc = keep.tile([P, T], U8, name="osc", align_bytes=64)
+        nc.vector.quantize_mx(out=ow[:].bitcast(FP8X4), scales=osc[:], in_=oq[:].rearrange("p c t -> p (c t)"))
+        nc.sync.dma_start(out_1[0].rearrange("p t d -> p (t d)").bitcast(I32), ow[:])
+        out_s = out_2[0].bitcast(I32)
+        for q in range(4):
+            queue = nc.sync if q % 2 else nc.scalar
+            queue.dma_start(out_s[4 * q : 4 * q + 4, :], osc[32 * q : 32 * q + 4, :].bitcast(I32))

@@ -1,6 +1,7 @@
 from contextlib import ExitStack
 
 import concourse.mybir as mybir
+from concourse.masks import make_identity
 
 K, T, E, C = 512, 512, 4, 256
 S = E * C
@@ -21,6 +22,7 @@ ADD = mybir.AluOpType.add
 GELU = mybir.ActivationFunctionType.Gelu_apprx_tanh
 COPY = mybir.ActivationFunctionType.Copy
 COLS = C // 16
+WIN = 2048
 
 
 def tile_moe_uni_gelu_kernel(
@@ -37,17 +39,18 @@ def tile_moe_uni_gelu_kernel(
             nc.sync.dma_start(tile[:], src)
             return tile
 
-        xs = keep.tile([P, T], U8, name="xs", align_bytes=64)
+        xs = keep.tile([P, WIN], U8, name="xs", align_bytes=64)
+        xw = keep.tile([P, WIN], I32, name="xw", tag="early", align_bytes=64)
         ws = keep.tile([P, E * K], U8, name="ws", align_bytes=64)
         nc.gpsimd.memset(xs[:].bitcast(I32), 0)
         nc.vector.memset(ws[:].bitcast(I32), 0)
+        nc.vector.memset(xw[:, T:], 0)
 
         offs_t = load_list("offs_t", offs)
-        xw = keep.tile([P, T], I32, name="xw", tag="early", align_bytes=64)
-        nc.sync.dma_start(xw[:], x_words[0].rearrange("p t d -> p (t d)").bitcast(I32))
+        nc.sync.dma_start(xw[:, :T], x_words[0].rearrange("p t d -> p (t d)").bitcast(I32))
         xs_rows = x_scales[0].bitcast(I32).rearrange("(q r) n -> r q n", r=4)
         for r in range(4):
-            nc.sync.dma_start(xs[r:P:32, :].bitcast(I32), xs_rows[r])
+            nc.sync.dma_start(xs[r:P:32, :T].bitcast(I32), xs_rows[r])
         ww = keep.tile([P, E * 2 * K], U8, name="ww", tag="late", align_bytes=64)
         nc.sync.dma_start(
             ww[:].bitcast(I32).rearrange("p (e n) -> p e n", e=E),
@@ -69,62 +72,97 @@ def tile_moe_uni_gelu_kernel(
             nc.vector.tensor_copy(wwp[t][:].bitcast(U16), ww[:].bitcast(U16).rearrange("p (m t) -> p m t", t=PACK)[:, :, t])
             nc.vector.tensor_copy(wsp[t][:], ws[:].rearrange("p (m t) -> p m t", t=PACK)[:, :, t])
 
-        def expert_plane(banks, y, words, scales, e, t):
-            acc = banks[t][e // 2][:, (e % 2) * C : (e % 2 + 1) * C]
+        ident = keep.tile([P, P], F32, name="ident")
+        make_identity(nc, ident[:])
+
+        def new_banks(step):
+            return [[psum.tile([P, 2, C], F32, name=f"mm{step}_{e}_{u}", tag=f"bank{e}_{u}") for u in range(2)] for e in range(E)]
+
+        def multiply(banks, words, scales, e, t):
             nc.tensor.matmul_mx(
-                out=acc,
+                out=banks[e][t // 2][:, t % 2, :],
                 lhsT=wwp[t][:, e * 2 * P : (e + 1) * 2 * P].bitcast(FP4X4),
                 lhsT_scale=wsp[t][:, e * P : (e + 1) * P],
-                rhs=words[:].bitcast(FP8X4),
-                rhs_scale=scales[:],
+                rhs=words[e].bitcast(FP8X4),
+                rhs_scale=scales[e],
                 start=True,
                 stop=True,
             )
-            nc.scalar.activation(y[t][:, e * C : (e + 1) * C], acc, GELU)
 
-        banks = [[psum.tile([P, 2 * C], F32, name=f"bank{t}_{h}") for h in range(2)] for t in range(PACK)]
+        def gelu(banks, dst, e, t):
+            nc.scalar.activation(dst[t][:, e * C : (e + 1) * C], banks[e][t // 2][:, t % 2, :], GELU)
 
-        gw = [keep.tile([P, C], U32, name=f"gw{e}", align_bytes=64) for e in range(E)]
-        gs = [keep.tile([P, C], U8, name=f"gs{e}", align_bytes=64) for e in range(E)]
+        def sum_turned(left, right, step, t):
+            acc = psum.tile([P, T], F32, name=f"acc{step}_{t}", tag=f"bank{2 * (t % 2)}_0")
+            for j in range(T // P):
+                blk = slice(j * P, (j + 1) * P)
+                nc.tensor.matmul(acc[:, blk], left[:, blk], ident[:], start=True, stop=False, is_transpose=True)
+                nc.tensor.matmul(acc[:, blk], right[:, blk], ident[:], start=False, stop=True, is_transpose=True)
+            turned = keep.tile([P, T], F32, name=f"turned{step}_{t}")
+            nc.scalar.copy(turned[:], acc[:])
+            return turned
+
+        def turn_back(turned, step, t):
+            back = psum.tile([P, T], F32, name=f"back{step}_{t}", tag=f"bank{2 * (t % 2) + 1}_0")
+            for j in range(T // P):
+                blk = slice(j * P, (j + 1) * P)
+                nc.tensor.transpose(back[:, blk], turned[:, blk], ident[:])
+            return back
+
+        gw_all = keep.tile([P, S], U32, name="gw_all", align_bytes=64)
+        gs_all = keep.tile([P, S], U8, name="gs_all", align_bytes=64)
+        gw = [gw_all[:, e * C : (e + 1) * C] for e in range(E)]
+        gs = [gs_all[:, e * C : (e + 1) * C] for e in range(E)]
         y = [keep.tile([P, S], F32, name=f"y{t}") for t in range(PACK)]
-        for e in range(E):
-            nc.vector.tensor_copy(gw[e][:], xw[:].bitcast(U32).indirect(offs_t[:, e * COLS : (e + 1) * COLS]))
+        nc.vector.tensor_copy(gw_all[:], xw[:].bitcast(U32).indirect(offs_t[:]))
         g1 = keep.tile([P, 2, T], F32, name="g1", tag="early", align_bytes=64)
         nc.sync.dma_start(g1[:], gate1.rearrange("r p t -> p r t"))
-        for e in range(E):
-            nc.vector.tensor_copy(gs[e][:], xs[:].indirect(offs_t[:, e * COLS : (e + 1) * COLS]))
-            if e < 2:
-                deal_weights(e)
-        deal_weights(2)
-        deal_weights(3)
+        nc.vector.tensor_copy(gs_all[:], xs[:].indirect(offs_t[:]))
+        for t in range(PACK):
+            deal_weights(t)
         g2 = keep.tile([P, 2, T], F32, name="g2", tag="late", align_bytes=64)
         nc.sync.dma_start(g2[:], gate2.rearrange("r p t -> p r t"))
-        for t in range(PACK):
-            for e in range(E):
-                expert_plane(banks, y, gw[e], gs[e], e, t)
+        banks = new_banks(1)
 
-        a = keep.tile([P, PACK, T], F32, name="a")
-        b = keep.tile([P, PACK, T], F32, name="b")
+        def plane(t, experts):
+            for e in experts:
+                multiply(banks, gw, gs, e, t)
+                gelu(banks, y, e, t)
+
+        a = [keep.tile([P, T], F32, name=f"a{t}") for t in range(2)]
+        b = [keep.tile([P, T], F32, name=f"b{t}") for t in range(2)]
+        ap = keep.tile([P, 2, T], F32, name="ap")
+        bp = keep.tile([P, 2, T], F32, name="bp")
         c_single = [keep.tile([P, T], BF16, name=f"c{t}", align_bytes=64) for t in range(2)]
         c_pair = keep.tile([P, T, 2], BF16, name="c_pair", align_bytes=64)
         xq = [keep.tile([P, C, PACK], BF16, name=f"xq{e}", align_bytes=64) for e in range(E)]
 
-        def first(dst, src, pos, gate, t):
-            nc.vector.tensor_tensor(dst[:, t, :], src[t][:].indirect(pos[:]), gate, MULT)
+        def fetch(dst, src, pos, gate):
+            nc.vector.tensor_tensor(dst, src[:].indirect(pos), gate, MULT)
 
-        def gather_single(t):
-            nc.vector.tensor_tensor(c_single[t][:], a[:, t, :], b[:, t, :], ADD)
-            for e in range(E):
-                nc.scalar.activation(xq[e][:, :, t], c_single[t][:].indirect(offs2_t[:, e * COLS : (e + 1) * COLS]), COPY)
+        def gather_single(e, t):
+            nc.scalar.activation(xq[e][:, :, t], c_single[t][:].indirect(offs2_t[:, e * COLS : (e + 1) * COLS]), COPY)
 
-        for t in range(PACK):
-            first(a, y, pos1_t, g1[:, 0, :], t)
-            if t in (1, 2):
-                gather_single(t - 1)
-            first(b, y, pos2_t, g1[:, 1, :], t)
-        nc.vector.tensor_tensor(
-            c_pair[:], a[:, 2:4, :].rearrange("p u t -> p t u"), b[:, 2:4, :].rearrange("p u t -> p t u"), ADD
-        )
+        for t in range(3):
+            plane(t, range(E))
+        for t in range(2):
+            fetch(a[t][:], y[t], pos1_t[:], g1[:, 0, :])
+            fetch(b[t][:], y[t], pos2_t[:], g1[:, 1, :])
+        turned0 = sum_turned(a[0], b[0], 1, 0)
+        plane(3, range(2))
+        nc.scalar.copy(c_single[0][:], turn_back(turned0, 1, 0)[:])
+        plane(3, range(2, E))
+        turned1 = sum_turned(a[1], b[1], 1, 1)
+        gather_single(0, 0)
+        nc.scalar.copy(c_single[1][:], turn_back(turned1, 1, 1)[:])
+        gather_single(0, 1)
+        for e in range(1, E):
+            gather_single(e, 0)
+            gather_single(e, 1)
+        for u in range(2):
+            fetch(ap[:, u, :], y[2 + u], pos1_t[:], g1[:, 0, :])
+            fetch(bp[:, u, :], y[2 + u], pos2_t[:], g1[:, 1, :])
+        nc.vector.tensor_tensor(c_pair[:], ap[:].rearrange("p u t -> p t u"), bp[:].rearrange("p u t -> p t u"), ADD)
 
         qw = [keep.tile([P, C], U32, name=f"qw{e}", align_bytes=64) for e in range(E)]
         qs = [keep.tile([P, C], U8, name=f"qs{e}", align_bytes=64) for e in range(E)]
@@ -140,38 +178,67 @@ def tile_moe_uni_gelu_kernel(
             if e > 0:
                 quantise(e - 1)
         quantise(E - 1)
-        for e in range(E - 1):
-            for t in range(PACK - 1):
-                expert_plane(banks, z, qw[e], qs[e], e, t)
-        for t in range(PACK - 1):
-            expert_plane(banks, z, qw[E - 1], qs[E - 1], E - 1, t)
+        banks2 = new_banks(2)
+        qw_ap = [tile[:] for tile in qw]
+        qs_ap = [tile[:] for tile in qs]
         for e in range(E):
-            expert_plane(banks, z, qw[e], qs[e], e, PACK - 1)
+            for t in range(2):
+                multiply(banks2, qw_ap, qs_ap, e, t)
+                if e == E - 1:
+                    gelu(banks2, z, e, t)
+            for t in range(2, PACK):
+                multiply(banks2, qw_ap, qs_ap, e, t)
+            if e < E - 1:
+                for t in range(2):
+                    gelu(banks2, z, e, t)
+        for t in range(2, PACK):
+            for e in range(E):
+                gelu(banks2, z, e, t)
 
-        a2 = keep.tile([P, PACK, T], F32, name="a2")
-        b2 = keep.tile([P, PACK, T], F32, name="b2")
-        o = [keep.tile([P, 2, T], F32, name=f"o{u}") for u in range(2)]
-        oq = keep.tile([P, T, PACK], BF16, name="oq", align_bytes=64)
-        out_rows = out_0.rearrange("(p t) n -> p t n", t=PACK)
-
-        def finish(t):
-            nc.vector.tensor_tensor(o[t // 2][:, t % 2, :], a2[:, t, :], b2[:, t, :], ADD)
-            nc.sync.dma_start(out_rows[:, t, :], o[t // 2][:, t % 2, :])
-
-        for t in range(PACK):
-            first(a2, z, pos3_t, g2[:, 0, :], t)
-            if t > 0:
-                finish(t - 1)
-            if t == 2:
-                nc.scalar.copy(oq[:, :, 0:2], o[0][:].rearrange("p u t -> p t u"))
-            first(b2, z, pos4_t, g2[:, 1, :], t)
-        finish(PACK - 1)
-        nc.vector.tensor_copy(oq[:, :, 2:4], o[1][:].rearrange("p u t -> p t u"))
-
-        ow = keep.tile([P, T], I32, name="ow", align_bytes=64)
+        H = T // 2
+        a2 = [keep.tile([P, T], F32, name=f"a2{t}") for t in range(2)]
+        b2 = [keep.tile([P, T], F32, name=f"b2{t}") for t in range(2)]
+        ah = [keep.tile([P, 2 * H], F32, name=f"ah{h}") for h in range(2)]
+        bh = [keep.tile([P, 2 * H], F32, name=f"bh{h}") for h in range(2)]
+        o_all = keep.tile([P, PACK, T], F32, name="o_all")
+        oq = [keep.tile([P, H, PACK], BF16, name=f"oq{h}", align_bytes=64) for h in range(2)]
+        ow = [keep.tile([P, H], I32, name=f"ow{h}", align_bytes=64) for h in range(2)]
         osc = keep.tile([P, T], U8, name="osc", align_bytes=64)
-        nc.vector.quantize_mx(out=ow[:].bitcast(FP8X4), scales=osc[:], in_=oq[:].rearrange("p c t -> p (c t)"))
-        nc.sync.dma_start(out_1[0].rearrange("p t d -> p (t d)").bitcast(I32), ow[:])
+        out_rows = out_0.rearrange("(p t) n -> p t n", t=PACK)
+        out_words = out_1[0].rearrange("p t d -> p (t d)").bitcast(I32)
+        half = [slice(h * H, (h + 1) * H) for h in range(2)]
+        half_list = [slice(h * H // 16, (h + 1) * H // 16) for h in range(2)]
+
+        def planes(h):
+            nc.vector.quantize_mx(out=ow[h][:].bitcast(FP8X4), scales=osc[:, half[h]], in_=oq[h][:].rearrange("p c t -> p (c t)"))
+            nc.sync.dma_start(out_words[:, half[h]], ow[h][:])
+
+        for t in range(2):
+            fetch(a2[t][:], z[t], pos3_t[:], g2[:, 0, :])
+            fetch(b2[t][:], z[t], pos4_t[:], g2[:, 1, :])
+        for h in range(2):
+            for u in range(2):
+                fetch(ah[h][:, half[u]], z[2 + u], pos3_t[:, half_list[h]], g2[:, 0, half[h]])
+                fetch(bh[h][:, half[u]], z[2 + u], pos4_t[:, half_list[h]], g2[:, 1, half[h]])
+        for t in range(2):
+            turned = sum_turned(a2[t], b2[t], 2, t)
+            nc.scalar.copy(o_all[:, t, :], turn_back(turned, 2, t)[:])
+            nc.sync.dma_start(out_rows[:, t, :], o_all[:, t, :])
+        nc.scalar.copy(oq[0][:, :, 0:2], o_all[:, 0:2, half[0]].rearrange("p u t -> p t u"))
+        back = turn_back(sum_turned(ah[0], bh[0], 2, 2), 2, 2)
+        nc.scalar.copy(oq[0][:, :, 2:4], back[:].rearrange("p (u t) -> p t u", u=2))
+        nc.scalar.copy(o_all[:, 2:4, half[0]], back[:].rearrange("p (u t) -> p u t", u=2))
+        nc.sync.dma_start(out_rows[:, 2:4, half[0]], o_all[:, 2:4, half[0]])
+
+        nc.vector.tensor_tensor(
+            o_all[:, 2:4, half[1]], ah[1][:].rearrange("p (u t) -> p u t", u=2), bh[1][:].rearrange("p (u t) -> p u t", u=2), ADD
+        )
+        nc.sync.dma_start(out_rows[:, 2:4, half[1]], o_all[:, 2:4, half[1]])
+        nc.vector.tensor_copy(
+            oq[1][:].rearrange("p (c i) t -> p c t i", i=4), o_all[:, :, half[1]].rearrange("p t (c i) -> p c t i", i=4)
+        )
+        planes(0)
+        planes(1)
         out_s = out_2[0].bitcast(I32)
         for q in range(4):
             queue = nc.sync if q % 2 else nc.scalar

@@ -23,6 +23,7 @@ GELU = mybir.ActivationFunctionType.Gelu_apprx_tanh
 COPY = mybir.ActivationFunctionType.Copy
 COLS = C // 16
 WIN = 2048
+BANK = 2048
 
 
 def tile_moe_uni_gelu_kernel(
@@ -32,6 +33,7 @@ def tile_moe_uni_gelu_kernel(
     with ExitStack() as ctx:
         lists = ctx.enter_context(tc.tile_pool(name="lists", bufs=1))
         keep = ctx.enter_context(tc.tile_pool(name="keep", bufs=1))
+        reuse = ctx.enter_context(tc.tile_pool(name="reuse", bufs=1))
         psum = ctx.enter_context(tc.psum_pool(name="psum", bufs=1))
 
         def load_list(name, src):
@@ -39,18 +41,17 @@ def tile_moe_uni_gelu_kernel(
             nc.sync.dma_start(tile[:], src)
             return tile
 
-        xs = keep.tile([P, WIN], U8, name="xs", align_bytes=64)
+        xs = reuse.tile([P, 3 * S], U8, name="xs", offset=0, align_bytes=64)
         xw = keep.tile([P, WIN], I32, name="xw", tag="early", align_bytes=64)
         ws = keep.tile([P, E * K], U8, name="ws", align_bytes=64)
-        nc.gpsimd.memset(xs[:].bitcast(I32), 0)
         nc.vector.memset(ws[:].bitcast(I32), 0)
+        nc.gpsimd.memset(xs[:, :S].bitcast(I32), 0)
         nc.vector.memset(xw[:, T:], 0)
+        c_pair = keep.tile([P, 2 * T], I32, name="c_pair", align_bytes=64)
+        nc.vector.memset(c_pair[:, T:], 0)
 
         offs_t = load_list("offs_t", offs)
         nc.sync.dma_start(xw[:, :T], x_words[0].rearrange("p t d -> p (t d)").bitcast(I32))
-        xs_rows = x_scales[0].bitcast(I32).rearrange("(q r) n -> r q n", r=4)
-        for r in range(4):
-            nc.sync.dma_start(xs[r:P:32, :T].bitcast(I32), xs_rows[r])
         ww = keep.tile([P, E * 2 * K], U8, name="ww", tag="late", align_bytes=64)
         nc.sync.dma_start(
             ww[:].bitcast(I32).rearrange("p (e n) -> p e n", e=E),
@@ -59,184 +60,225 @@ def tile_moe_uni_gelu_kernel(
         ws_rows = w_scales.bitcast(I32).rearrange("e s (q r) n -> r q (e s) n", r=4)
         for r in range(4):
             nc.sync.dma_start(ws[r:P:32, :].bitcast(I32).rearrange("q (e n) -> q e n", e=E), ws_rows[r])
+        xs_rows = x_scales[0].bitcast(I32).rearrange("(q r) n -> r q n", r=4)
+        for r in range(4):
+            nc.sync.dma_start(xs[r:P:32, :T].bitcast(I32), xs_rows[r])
         pos1_t = load_list("pos1_t", pos1)
         pos2_t = load_list("pos2_t", pos2)
         offs2_t = load_list("offs2_t", offs2)
         pos3_t = load_list("pos3_t", pos3)
         pos4_t = load_list("pos4_t", pos4)
 
-        wwp = [keep.tile([P, E * 2 * P], U8, name=f"wwp{t}", align_bytes=64) for t in range(PACK)]
-        wsp = [keep.tile([P, E * P], U8, name=f"wsp{t}", align_bytes=64) for t in range(PACK)]
+        wwp = []
+        wsp = []
 
         def deal_weights(t):
+            if t < 2:
+                wwp.append(keep.tile([P, E * 2 * P], U8, name=f"wwp{t}", align_bytes=64))
+                wsp.append(keep.tile([P, E * P], U8, name=f"wsp{t}", align_bytes=64))
+            else:
+                wwp.append(reuse.tile([P, E * 2 * P], U8, name=f"wwp{t}", offset=(t - 2) * 3 * E * P, align_bytes=64))
+                wsp.append(reuse.tile([P, E * P], U8, name=f"wsp{t}", offset=((t - 2) * 3 + 2) * E * P, align_bytes=64))
             nc.vector.tensor_copy(wwp[t][:].bitcast(U16), ww[:].bitcast(U16).rearrange("p (m t) -> p m t", t=PACK)[:, :, t])
             nc.vector.tensor_copy(wsp[t][:], ws[:].rearrange("p (m t) -> p m t", t=PACK)[:, :, t])
 
         ident = keep.tile([P, P], F32, name="ident")
         make_identity(nc, ident[:])
+        ident_bf = keep.tile([P, P], BF16, name="ident_bf")
+        make_identity(nc, ident_bf[:])
 
-        def new_banks(step):
-            return [[psum.tile([P, 2, C], F32, name=f"mm{step}_{e}_{u}", tag=f"bank{e}_{u}") for u in range(2)] for e in range(E)]
+        H = T // 2
+        half = [slice(h * H, (h + 1) * H) for h in range(2)]
+        half_list = [slice(h * H // 16, (h + 1) * H // 16) for h in range(2)]
 
-        def multiply(banks, words, scales, e, t):
+        def bank(name, k, dtype=F32):
+            return psum.tile([P, 2 * C], dtype, name=name, offset=k * BANK)[:]
+
+        def six_banks(name):
+            return [bank(f"{name}_{k}", k) for k in range(2, 8)]
+
+        def multiply(dst, words, scales, e, t):
             nc.tensor.matmul_mx(
-                out=banks[e][t // 2][:, t % 2, :],
+                out=dst,
                 lhsT=wwp[t][:, e * 2 * P : (e + 1) * 2 * P].bitcast(FP4X4),
                 lhsT_scale=wsp[t][:, e * P : (e + 1) * P],
-                rhs=words[e].bitcast(FP8X4),
-                rhs_scale=scales[e],
+                rhs=words.bitcast(FP8X4),
+                rhs_scale=scales,
                 start=True,
                 stop=True,
             )
 
-        def gelu(banks, dst, e, t):
-            nc.scalar.activation(dst[t][:, e * C : (e + 1) * C], banks[e][t // 2][:, t % 2, :], GELU)
-
-        def sum_turned(left, right, step, t):
-            acc = psum.tile([P, T], F32, name=f"acc{step}_{t}", tag=f"bank{2 * (t % 2)}_0")
-            for j in range(T // P):
-                blk = slice(j * P, (j + 1) * P)
-                nc.tensor.matmul(acc[:, blk], left[:, blk], ident[:], start=True, stop=False, is_transpose=True)
-                nc.tensor.matmul(acc[:, blk], right[:, blk], ident[:], start=False, stop=True, is_transpose=True)
-            turned = keep.tile([P, T], F32, name=f"turned{step}_{t}")
-            nc.scalar.copy(turned[:], acc[:])
+        def sum_turned(left, right, name, acc, dtype=F32):
+            blocks = [slice(j * P, (j + 1) * P) for j in range(T // P)]
+            for j, blk in enumerate(blocks):
+                nc.tensor.matmul(acc[:, blk], left[:, blk], ident[:], start=(j == 0), stop=False, is_transpose=True)
+            for j, blk in enumerate(blocks):
+                nc.tensor.matmul(acc[:, blk], right[:, blk], ident[:], start=False, stop=(j == len(blocks) - 1), is_transpose=True)
+            turned = keep.tile([P, T], dtype, name=f"turned{name}", tag=f"turned{name}", align_bytes=64)
+            nc.scalar.copy(turned[:], acc)
             return turned
 
-        def turn_back(turned, step, t):
-            back = psum.tile([P, T], F32, name=f"back{step}_{t}", tag=f"bank{2 * (t % 2) + 1}_0")
+        def turn_back(turned, back, identity=ident):
             for j in range(T // P):
                 blk = slice(j * P, (j + 1) * P)
-                nc.tensor.transpose(back[:, blk], turned[:, blk], ident[:])
+                nc.tensor.transpose(back[:, blk], turned[:, blk], identity[:])
             return back
-
-        gw_all = keep.tile([P, S], U32, name="gw_all", align_bytes=64)
-        gs_all = keep.tile([P, S], U8, name="gs_all", align_bytes=64)
-        gw = [gw_all[:, e * C : (e + 1) * C] for e in range(E)]
-        gs = [gs_all[:, e * C : (e + 1) * C] for e in range(E)]
-        y = [keep.tile([P, S], F32, name=f"y{t}") for t in range(PACK)]
-        nc.vector.tensor_copy(gw_all[:], xw[:].bitcast(U32).indirect(offs_t[:]))
-        g1 = keep.tile([P, 2, T], F32, name="g1", tag="early", align_bytes=64)
-        nc.sync.dma_start(g1[:], gate1.rearrange("r p t -> p r t"))
-        nc.vector.tensor_copy(gs_all[:], xs[:].indirect(offs_t[:]))
-        for t in range(PACK):
-            deal_weights(t)
-        g2 = keep.tile([P, 2, T], F32, name="g2", tag="late", align_bytes=64)
-        nc.sync.dma_start(g2[:], gate2.rearrange("r p t -> p r t"))
-        banks = new_banks(1)
-
-        def plane(t, experts):
-            for e in experts:
-                multiply(banks, gw, gs, e, t)
-                gelu(banks, y, e, t)
-
-        a = [keep.tile([P, T], F32, name=f"a{t}") for t in range(2)]
-        b = [keep.tile([P, T], F32, name=f"b{t}") for t in range(2)]
-        ap = keep.tile([P, 2, T], F32, name="ap")
-        bp = keep.tile([P, 2, T], F32, name="bp")
-        c_single = [keep.tile([P, T], BF16, name=f"c{t}", align_bytes=64) for t in range(2)]
-        c_pair = keep.tile([P, T, 2], BF16, name="c_pair", align_bytes=64)
-        xq = [keep.tile([P, C, PACK], BF16, name=f"xq{e}", align_bytes=64) for e in range(E)]
 
         def fetch(dst, src, pos, gate):
             nc.vector.tensor_tensor(dst, src[:].indirect(pos), gate, MULT)
 
-        def gather_single(e, t):
-            nc.scalar.activation(xq[e][:, :, t], c_single[t][:].indirect(offs2_t[:, e * COLS : (e + 1) * COLS]), COPY)
-
-        for t in range(3):
-            plane(t, range(E))
-        for t in range(2):
-            fetch(a[t][:], y[t], pos1_t[:], g1[:, 0, :])
-            fetch(b[t][:], y[t], pos2_t[:], g1[:, 1, :])
-        turned0 = sum_turned(a[0], b[0], 1, 0)
-        plane(3, range(2))
-        nc.scalar.copy(c_single[0][:], turn_back(turned0, 1, 0)[:])
-        plane(3, range(2, E))
-        turned1 = sum_turned(a[1], b[1], 1, 1)
-        gather_single(0, 0)
-        nc.scalar.copy(c_single[1][:], turn_back(turned1, 1, 1)[:])
-        gather_single(0, 1)
-        for e in range(1, E):
-            gather_single(e, 0)
-            gather_single(e, 1)
-        for u in range(2):
-            fetch(ap[:, u, :], y[2 + u], pos1_t[:], g1[:, 0, :])
-            fetch(bp[:, u, :], y[2 + u], pos2_t[:], g1[:, 1, :])
-        nc.vector.tensor_tensor(c_pair[:], ap[:].rearrange("p u t -> p t u"), bp[:].rearrange("p u t -> p t u"), ADD)
-
-        qw = [keep.tile([P, C], U32, name=f"qw{e}", align_bytes=64) for e in range(E)]
-        qs = [keep.tile([P, C], U8, name=f"qs{e}", align_bytes=64) for e in range(E)]
-        z = [keep.tile([P, S], F32, name=f"z{t}") for t in range(PACK)]
-        c_words = c_pair[:].rearrange("p t u -> p (t u)").bitcast(U32)
-
-        def quantise(e):
-            nc.vector.quantize_mx(out=qw[e][:].bitcast(FP8X4), scales=qs[e][:], in_=xq[e][:].rearrange("p c t -> p (c t)"))
-
-        for e in range(E):
-            dst = xq[e][:].rearrange("p c t -> p (c t)").bitcast(U32).rearrange("p (c u) -> p c u", u=2)[:, :, 1]
-            nc.vector.tensor_copy(dst, c_words.indirect(offs2_t[:, e * COLS : (e + 1) * COLS]))
-            if e > 0:
-                quantise(e - 1)
-        quantise(E - 1)
-        banks2 = new_banks(2)
-        qw_ap = [tile[:] for tile in qw]
-        qs_ap = [tile[:] for tile in qs]
-        for e in range(E):
+        def fetch_all(src, pos_a, pos_b, gate, step, cuts, first_sum=None):
+            widths = [T, T] + [2 * (hi - lo) for lo, hi in cuts]
+            a = [keep.tile([P, w], F32, name=f"a{step}_{j}") for j, w in enumerate(widths)]
+            b = [keep.tile([P, w], F32, name=f"b{step}_{j}") for j, w in enumerate(widths)]
             for t in range(2):
-                multiply(banks2, qw_ap, qs_ap, e, t)
-                if e == E - 1:
-                    gelu(banks2, z, e, t)
-            for t in range(2, PACK):
-                multiply(banks2, qw_ap, qs_ap, e, t)
-            if e < E - 1:
-                for t in range(2):
-                    gelu(banks2, z, e, t)
-        for t in range(2, PACK):
-            for e in range(E):
-                gelu(banks2, z, e, t)
+                fetch(a[t][:], src[t], pos_a[:], gate[:, 0, :])
+                fetch(b[t][:], src[t], pos_b[:], gate[:, 1, :])
+            for h, (lo, hi) in enumerate(cuts):
+                w, entries, tokens = hi - lo, slice(lo // 16, hi // 16), slice(lo, hi)
+                for u in range(2):
+                    fetch(a[2 + h][:, u * w : (u + 1) * w], src[2 + u], pos_a[:, entries], gate[:, 0, tokens])
+                    if (h, u) == (1, 0):
+                        nc.vector.tensor_tensor(first_sum, a[2][:], b[2][:], ADD)
+                    fetch(b[2 + h][:, u * w : (u + 1) * w], src[2 + u], pos_b[:, entries], gate[:, 1, tokens])
+            return a, b
 
-        H = T // 2
-        a2 = [keep.tile([P, T], F32, name=f"a2{t}") for t in range(2)]
-        b2 = [keep.tile([P, T], F32, name=f"b2{t}") for t in range(2)]
-        ah = [keep.tile([P, 2 * H], F32, name=f"ah{h}") for h in range(2)]
-        bh = [keep.tile([P, 2 * H], F32, name=f"bh{h}") for h in range(2)]
-        o_all = keep.tile([P, PACK, T], F32, name="o_all")
+        gw = keep.tile([P, S], U32, name="gw", align_bytes=64)
+        gs = [keep.tile([P, 2 * C], U8, name=f"gs{h}", align_bytes=64) for h in range(2)]
+        y = [keep.tile([P, S], F32, name=f"y{t}") for t in range(PACK)]
+        nc.vector.tensor_copy(gw[:], xw[:].bitcast(U32).indirect(offs_t[:]))
+        g1 = keep.tile([P, 2, T], F32, name="g1", tag="early", align_bytes=64)
+        nc.sync.dma_start(g1[:], gate1.rearrange("r p t -> p r t"))
+        deal_weights(0)
+        deal_weights(1)
+        for h in range(2):
+            nc.vector.tensor_copy(gs[h][:], xs[:, :S].indirect(offs_t[:, 2 * h * COLS : 2 * (h + 1) * COLS]))
+        deal_weights(2)
+        deal_weights(3)
+        g2 = keep.tile([P, 2, T], F32, name="g2", tag="late", align_bytes=64)
+        nc.sync.dma_start(g2[:], gate2.rearrange("r p t -> p r t"))
+
+        def first_step(acc, t, h):
+            for u in range(2):
+                e = 2 * h + u
+                multiply(acc[:, half[u]], gw[:, e * C : (e + 1) * C], gs[h][:, half[u]], e, t)
+            nc.scalar.activation(y[t][:, 2 * h * C : 2 * (h + 1) * C], acc, GELU)
+
+        first_step(bank("mm1_0", 0), 0, 0)
+        first_step(psum.tile([P, 2 * 2 * C], F32, name="mm1_1", offset=BANK)[:, : 2 * C], 0, 1)
+        banks = six_banks("mm1")
+        for t in range(1, PACK):
+            for h in range(2):
+                first_step(banks[2 * (t - 1) + 1 - h], t, 1 - h)
+
+        a, b = fetch_all(y, pos1_t, pos2_t, g1, 1, [(0, T)])
+        c_single = [keep.tile([P, T], BF16, name=f"c{t}", align_bytes=64) for t in range(2)]
+        c_pair_bf = c_pair[:, :T].bitcast(BF16)
+        both = [keep.tile([P, 2 * C], I32, name=f"both{e}", align_bytes=64) for e in range(2)]
+
+        def gather_single(dst_words, e, t):
+            dst = dst_words.bitcast(BF16).rearrange("p (c u) -> p c u", u=2)[:, :, t]
+            nc.scalar.activation(dst, c_single[t][:].indirect(offs2_t[:, e * COLS : (e + 1) * COLS]), COPY)
+
+        turned = [sum_turned(a[t], b[t], f"1{t}", bank(f"acc1{t}", 2 * t), BF16) for t in range(2)]
+        nc.scalar.copy(c_single[0][:], turn_back(turned[0], bank("back10", 1, BF16), ident_bf))
+        gather_single(both[0][:, :C], 0, 0)
+        nc.scalar.copy(c_single[1][:], turn_back(turned[1], bank("back11", 3, BF16), ident_bf))
+        gather_single(both[1][:, :C], 1, 0)
+        gather_single(both[0][:, :C], 0, 1)
+        gather_single(both[1][:, :C], 1, 1)
+        both23 = keep.tile([P, 4 * C], I32, name="both23", tag="turned11", align_bytes=64)
+        for e in range(2, E):
+            for t in range(2):
+                gather_single(both23[:, (e - 2) * C : (e - 1) * C], e, t)
+        nc.vector.tensor_tensor(
+            c_pair_bf.rearrange("p (t u) -> p t u", u=2),
+            a[2][:].rearrange("p (u t) -> p t u", u=2),
+            b[2][:].rearrange("p (u t) -> p t u", u=2),
+            ADD,
+        )
+
+        groups = [(0, 1, both[0][:]), (2, 2, both23[:]), (1, 1, both[1][:])]
+        xq = [keep.tile([P, n * C * PACK], BF16, name=f"xq{e}", align_bytes=64) for e, n, src in groups]
+        qw = [keep.tile([P, n * C], U32, name=f"qw{e}", tag=f"qw{e}", align_bytes=64) for e, n, src in groups]
+        qs = [keep.tile([P, n * C], U8, name=f"qs{e}", tag=f"qs{e}", align_bytes=64) for e, n, src in groups]
+
+        def gather_pair(g):
+            e, n, src = groups[g]
+            nc.vector.tensor_copy(src[:, n * C :].bitcast(U32), c_pair[:].bitcast(U32).indirect(offs2_t[:, e * COLS : (e + n) * COLS]))
+
+        def weave(g, copy):
+            dst = xq[g][:].bitcast(U32).rearrange("p (c u) -> p c u", u=2)
+            copy(dst, groups[g][2].bitcast(U32).rearrange("p (u c) -> p c u", u=2))
+
+        def quantise(g):
+            nc.vector.quantize_mx(out=qw[g][:].bitcast(FP8X4), scales=qs[g][:], in_=xq[g][:])
+
+        gather_pair(0)
+        gather_pair(2)
+        gather_pair(1)
+        weave(0, nc.scalar.copy)
+        weave(2, nc.scalar.copy)
+        dst = xq[1][:].bitcast(I32).rearrange("p (c u) -> p c u", u=2)
+        nc.vector.tensor_copy(dst, both23[:].rearrange("p (u c) -> p c u", u=2))
+        quantise(0)
+        quantise(1)
+        quantise(2)
+
+        z = [keep.tile([P, S], F32, name=f"z{t}", align_bytes=64) for t in range(PACK)]
+        operands = [(qw[0][:], qs[0][:]), (qw[2][:], qs[2][:]), (qw[1][:, half[0]], qs[1][:, half[0]]), (qw[1][:, half[1]], qs[1][:, half[1]])]
+        wide = psum.tile([P, 6 * 2 * C], F32, name="mm2_last", offset=2 * BANK)
+        banks = [bank("mm2_pair", 0), bank("mm2_third", 1), wide[:, : 2 * C]]
+        for g, (e0, n, src) in enumerate(groups):
+            for e in range(e0, e0 + n):
+                multiply(banks[g][:, half[e - e0]], *operands[e], e, 0)
+            nc.scalar.activation(z[0][:, e0 * C : (e0 + n) * C], banks[g][:, : n * C], GELU)
+        banks = six_banks("mm2_rest")
+        for t in range(1, PACK):
+            for e in range(E):
+                multiply(banks[2 * (t - 1) + e // 2][:, half[e % 2]], *operands[e], e, t)
+        for t in range(1, PACK):
+            for h in range(2):
+                nc.scalar.activation(z[t][:, 2 * h * C : 2 * (h + 1) * C], banks[2 * (t - 1) + h], GELU)
+
+        cuts = [(0, H), (H, H + P), (H + P, T)]
+        o_first = keep.tile([P, PACK * H], F32, name="o_first")
+        a2, b2 = fetch_all(z, pos3_t, pos4_t, g2, 2, cuts, o_first[:, 2 * H :])
+        o_low = keep.tile([P, 2 * H], F32, name="o_low")
+        o_high = keep.tile([P, 2 * H], F32, name="o_high")
         oq = [keep.tile([P, H, PACK], BF16, name=f"oq{h}", align_bytes=64) for h in range(2)]
         ow = [keep.tile([P, H], I32, name=f"ow{h}", align_bytes=64) for h in range(2)]
         osc = keep.tile([P, T], U8, name="osc", align_bytes=64)
         out_rows = out_0.rearrange("(p t) n -> p t n", t=PACK)
         out_words = out_1[0].rearrange("p t d -> p (t d)").bitcast(I32)
-        half = [slice(h * H, (h + 1) * H) for h in range(2)]
-        half_list = [slice(h * H // 16, (h + 1) * H // 16) for h in range(2)]
 
         def planes(h):
             nc.vector.quantize_mx(out=ow[h][:].bitcast(FP8X4), scales=osc[:, half[h]], in_=oq[h][:].rearrange("p c t -> p (c t)"))
             nc.sync.dma_start(out_words[:, half[h]], ow[h][:])
 
+        turned = [sum_turned(a2[t], b2[t], f"2{t}", bank(f"acc2{t}", 2 * t)) for t in range(2)]
         for t in range(2):
-            fetch(a2[t][:], z[t], pos3_t[:], g2[:, 0, :])
-            fetch(b2[t][:], z[t], pos4_t[:], g2[:, 1, :])
-        for h in range(2):
-            for u in range(2):
-                fetch(ah[h][:, half[u]], z[2 + u], pos3_t[:, half_list[h]], g2[:, 0, half[h]])
-                fetch(bh[h][:, half[u]], z[2 + u], pos4_t[:, half_list[h]], g2[:, 1, half[h]])
-        for t in range(2):
-            turned = sum_turned(a2[t], b2[t], 2, t)
-            nc.scalar.copy(o_all[:, t, :], turn_back(turned, 2, t)[:])
-            nc.sync.dma_start(out_rows[:, t, :], o_all[:, t, :])
-        nc.scalar.copy(oq[0][:, :, 0:2], o_all[:, 0:2, half[0]].rearrange("p u t -> p t u"))
-        back = turn_back(sum_turned(ah[0], bh[0], 2, 2), 2, 2)
-        nc.scalar.copy(oq[0][:, :, 2:4], back[:].rearrange("p (u t) -> p t u", u=2))
-        nc.scalar.copy(o_all[:, 2:4, half[0]], back[:].rearrange("p (u t) -> p u t", u=2))
-        nc.sync.dma_start(out_rows[:, 2:4, half[0]], o_all[:, 2:4, half[0]])
-
-        nc.vector.tensor_tensor(
-            o_all[:, 2:4, half[1]], ah[1][:].rearrange("p (u t) -> p u t", u=2), bh[1][:].rearrange("p (u t) -> p u t", u=2), ADD
+            back = turn_back(turned[t], bank(f"back2{t}", 2 * t + 1))
+            nc.scalar.copy(o_first[:, t * H : (t + 1) * H], back[:, half[0]])
+            nc.scalar.copy(o_low[:, half[t]], back[:, half[1]])
+        nc.sync.dma_start(out_rows[:, :, half[0]], o_first[:].rearrange("p (t n) -> p t n", t=PACK))
+        nc.sync.dma_start(out_rows[:, 0:2, half[1]], o_low[:].rearrange("p (t n) -> p t n", t=2))
+        nc.scalar.copy(
+            oq[0][:].rearrange("p (c i) t -> p c t i", i=4), o_first[:].rearrange("p (t c i) -> p c t i", t=PACK, i=4)
         )
-        nc.sync.dma_start(out_rows[:, 2:4, half[1]], o_all[:, 2:4, half[1]])
-        nc.vector.tensor_copy(
-            oq[1][:].rearrange("p (c i) t -> p c t i", i=4), o_all[:, :, half[1]].rearrange("p t (c i) -> p c t i", i=4)
-        )
+        nc.scalar.copy(oq[1][:, :, 0:2], o_low[:].rearrange("p (u t) -> p t u", u=2))
+        high = o_high[:].rearrange("p (u t) -> p u t", u=2)
+        for j in range(2):
+            nc.vector.tensor_tensor(
+                high[:, :, j * P : (j + 1) * P],
+                a2[3 + j][:].rearrange("p (u t) -> p u t", u=2),
+                b2[3 + j][:].rearrange("p (u t) -> p u t", u=2),
+                ADD,
+            )
+        nc.sync.dma_start(out_rows[:, 2:4, half[1]], high)
+        for j in range(2):
+            tokens = slice(j * P, (j + 1) * P)
+            nc.vector.tensor_copy(oq[1][:, tokens, 2:4], high[:, :, tokens].rearrange("p u t -> p t u"))
         planes(0)
         planes(1)
         out_s = out_2[0].bitcast(I32)

@@ -192,9 +192,9 @@ def tile_moe_uni_gelu_kernel(
             for t in range(2):
                 gather_single(both23[:, (e - 2) * C : (e - 1) * C], e, t)
         nc.vector.tensor_tensor(
-            c_pair_bf.rearrange("p (t u) -> p t u", u=2),
-            a[2][:].rearrange("p (u t) -> p t u", u=2),
-            b[2][:].rearrange("p (u t) -> p t u", u=2),
+            c_pair_bf.rearrange("p (c i u) -> p c u i", i=4, u=2),
+            a[2][:].rearrange("p (u c i) -> p c u i", u=2, i=4),
+            b[2][:].rearrange("p (u c i) -> p c u i", u=2, i=4),
             ADD,
         )
 
@@ -244,8 +244,7 @@ def tile_moe_uni_gelu_kernel(
         cuts = [(0, H), (H, H + P), (H + P, T)]
         o_first = keep.tile([P, PACK * H], F32, name="o_first")
         a2, b2 = fetch_all(z, pos3_t, pos4_t, g2, 2, cuts, o_first[:, 2 * H :])
-        o_low = keep.tile([P, 2 * H], F32, name="o_low")
-        o_high = keep.tile([P, 2 * H], F32, name="o_high")
+        o_second = keep.tile([P, PACK * H], F32, name="o_second")
         oq = [keep.tile([P, H, PACK], BF16, name=f"oq{h}", align_bytes=64) for h in range(2)]
         ow = [keep.tile([P, H], I32, name=f"ow{h}", align_bytes=64) for h in range(2)]
         osc = keep.tile([P, T], U8, name="osc", align_bytes=64)
@@ -260,25 +259,28 @@ def tile_moe_uni_gelu_kernel(
         for t in range(2):
             back = turn_back(turned[t], bank(f"back2{t}", 2 * t + 1))
             nc.scalar.copy(o_first[:, t * H : (t + 1) * H], back[:, half[0]])
-            nc.scalar.copy(o_low[:, half[t]], back[:, half[1]])
-        nc.sync.dma_start(out_rows[:, :, half[0]], o_first[:].rearrange("p (t n) -> p t n", t=PACK))
-        nc.sync.dma_start(out_rows[:, 0:2, half[1]], o_low[:].rearrange("p (t n) -> p t n", t=2))
+            nc.scalar.copy(o_second[:, t * H : (t + 1) * H], back[:, half[1]])
+        first = o_first[:].rearrange("p (t n) -> p t n", t=PACK)
+        second = o_second[:].rearrange("p (t n) -> p t n", t=PACK)
+        nc.scalar.dma_start(out_rows[:, 0:2, half[0]], first[:, 0:2, :])
+        nc.scalar.dma_start(out_rows[:, 0:2, half[1]], second[:, 0:2, :])
+        nc.sync.dma_start(out_rows[:, 2:4, half[0]], first[:, 2:4, :])
         nc.scalar.copy(
             oq[0][:].rearrange("p (c i) t -> p c t i", i=4), o_first[:].rearrange("p (t c i) -> p c t i", t=PACK, i=4)
         )
-        nc.scalar.copy(oq[1][:, :, 0:2], o_low[:].rearrange("p (u t) -> p t u", u=2))
-        high = o_high[:].rearrange("p (u t) -> p u t", u=2)
         for j in range(2):
             nc.vector.tensor_tensor(
-                high[:, :, j * P : (j + 1) * P],
+                second[:, 2:4, j * P : (j + 1) * P],
                 a2[3 + j][:].rearrange("p (u t) -> p u t", u=2),
                 b2[3 + j][:].rearrange("p (u t) -> p u t", u=2),
                 ADD,
             )
-        nc.sync.dma_start(out_rows[:, 2:4, half[1]], high)
+        nc.sync.dma_start(out_rows[:, 2:4, half[1]], second[:, 2:4, :])
         for j in range(2):
             tokens = slice(j * P, (j + 1) * P)
-            nc.vector.tensor_copy(oq[1][:, tokens, 2:4], high[:, :, tokens].rearrange("p u t -> p t u"))
+            nc.vector.tensor_copy(
+                oq[1][:, tokens, :].rearrange("p (c i) t -> p c t i", i=4), second[:, :, tokens].rearrange("p t (c i) -> p c t i", i=4)
+            )
         planes(0)
         planes(1)
         out_s = out_2[0].bitcast(I32)

@@ -7,6 +7,10 @@ K, T, E, C = 512, 512, 4, 256
 S = E * C
 P = 128
 PACK = 4
+H = T // 2
+ENTRIES = 16
+BANK = 2048
+RUN = 4
 FLOPS = 2 * 2 * K * K * S
 
 F32 = mybir.dt.float32
@@ -21,9 +25,14 @@ MULT = mybir.AluOpType.mult
 ADD = mybir.AluOpType.add
 GELU = mybir.ActivationFunctionType.Gelu_apprx_tanh
 COPY = mybir.ActivationFunctionType.Copy
-COLS = C // 16
-WIN = 2048
-BANK = 2048
+
+
+def part(index, width):
+    return slice(index * width, (index + 1) * width)
+
+
+def entries(offsets, lo, hi):
+    return offsets[:, lo // ENTRIES : hi // ENTRIES]
 
 
 def tile_moe_uni_gelu_kernel(
@@ -36,254 +45,249 @@ def tile_moe_uni_gelu_kernel(
         reuse = ctx.enter_context(tc.tile_pool(name="reuse", bufs=1))
         psum = ctx.enter_context(tc.psum_pool(name="psum", bufs=1))
 
-        def load_list(name, src):
-            tile = lists.tile(list(src.shape), U16, name=name)
-            nc.sync.dma_start(tile[:], src)
+        def load_list(name, source):
+            tile = lists.tile(list(source.shape), U16, name=name)
+            nc.sync.dma_start(tile[:], source)
             return tile
 
-        xs = reuse.tile([P, 3 * S], U8, name="xs", offset=0, align_bytes=64)
-        xw = keep.tile([P, WIN], I32, name="xw", tag="early", align_bytes=64)
-        ws = keep.tile([P, E * K], U8, name="ws", align_bytes=64)
-        nc.vector.memset(ws[:].bitcast(I32), 0)
-        nc.gpsimd.memset(xs[:, :S].bitcast(I32), 0)
-        nc.vector.memset(xw[:, T:], 0)
-        c_pair = keep.tile([P, 2 * T], I32, name="c_pair", align_bytes=64)
-        nc.vector.memset(c_pair[:, T:], 0)
+        def bank(name, first, dtype=F32, span=1):
+            return psum.tile([P, span * 2 * C], dtype, name=name, offset=first * BANK)[:, : 2 * C]
 
-        offs_t = load_list("offs_t", offs)
-        nc.sync.dma_start(xw[:, :T], x_words[0].rearrange("p t d -> p (t d)").bitcast(I32))
-        ww = keep.tile([P, E * 2 * K], U8, name="ww", tag="late", align_bytes=64)
+        x_scale_tile = reuse.tile([P, 3 * S], U8, name="x_scale_tile", offset=0, align_bytes=64)
+        x_scale_window = x_scale_tile[:, : 2 * T]
+        x_window = keep.tile([P, 2 * S], I32, name="x_window", tag="x_then_gate1", align_bytes=64)
+        w_scale_tile = keep.tile([P, E * K], U8, name="w_scale_tile", align_bytes=64)
+        nc.vector.memset(w_scale_tile[:].bitcast(I32), 0)
+        nc.gpsimd.memset(x_scale_window.bitcast(I32), 0)
+        nc.vector.memset(x_window[:, T:], 0)
+        c_pairs = keep.tile([P, 2 * T], I32, name="c_pairs", align_bytes=64)
+        nc.vector.memset(c_pairs[:, T:], 0)
+
+        offs_tile = load_list("offs_tile", offs)
+        nc.sync.dma_start(x_window[:, :T], x_words[0].rearrange("p t d -> p (t d)").bitcast(I32))
+        w_word_tile = keep.tile([P, E * 2 * K], U8, name="w_word_tile", tag="w_then_gate2", align_bytes=64)
         nc.sync.dma_start(
-            ww[:].bitcast(I32).rearrange("p (e n) -> p e n", e=E),
+            w_word_tile[:].bitcast(I32).rearrange("p (e n) -> p e n", e=E),
             w_words.rearrange("e s p n -> p (e s) n").bitcast(I32),
         )
-        ws_rows = w_scales.bitcast(I32).rearrange("e s (q r) n -> r q (e s) n", r=4)
+        w_scale_rows = w_scales.bitcast(I32).rearrange("e s (q r) n -> r q (e s) n", r=4)
         for r in range(4):
-            nc.sync.dma_start(ws[r:P:32, :].bitcast(I32).rearrange("q (e n) -> q e n", e=E), ws_rows[r])
-        xs_rows = x_scales[0].bitcast(I32).rearrange("(q r) n -> r q n", r=4)
+            nc.sync.dma_start(w_scale_tile[r:P:32, :].bitcast(I32).rearrange("q (e n) -> q e n", e=E), w_scale_rows[r])
+        x_scale_rows = x_scales[0].bitcast(I32).rearrange("(q r) n -> r q n", r=4)
         for r in range(4):
-            nc.sync.dma_start(xs[r:P:32, :T].bitcast(I32), xs_rows[r])
-        pos1_t = load_list("pos1_t", pos1)
-        pos2_t = load_list("pos2_t", pos2)
-        offs2_t = load_list("offs2_t", offs2)
-        pos3_t = load_list("pos3_t", pos3)
-        pos4_t = load_list("pos4_t", pos4)
+            nc.sync.dma_start(x_scale_tile[r:P:32, :T].bitcast(I32), x_scale_rows[r])
+        pos1_tile = load_list("pos1_tile", pos1)
+        pos2_tile = load_list("pos2_tile", pos2)
+        offs2_tile = load_list("offs2_tile", offs2)
+        pos3_tile = load_list("pos3_tile", pos3)
+        pos4_tile = load_list("pos4_tile", pos4)
 
-        wwp = []
-        wsp = []
+        identity = keep.tile([P, P], F32, name="identity")
+        make_identity(nc, identity[:])
+        identity_bf16 = keep.tile([P, P], BF16, name="identity_bf16")
+        make_identity(nc, identity_bf16[:])
 
-        def deal_weights(t):
-            if t < 2:
-                wwp.append(keep.tile([P, E * 2 * P], U8, name=f"wwp{t}", align_bytes=64))
-                wsp.append(keep.tile([P, E * P], U8, name=f"wsp{t}", align_bytes=64))
-            else:
-                wwp.append(reuse.tile([P, E * 2 * P], U8, name=f"wwp{t}", offset=(t - 2) * 3 * E * P, align_bytes=64))
-                wsp.append(reuse.tile([P, E * P], U8, name=f"wsp{t}", offset=((t - 2) * 3 + 2) * E * P, align_bytes=64))
-            nc.vector.tensor_copy(wwp[t][:].bitcast(U16), ww[:].bitcast(U16).rearrange("p (m t) -> p m t", t=PACK)[:, :, t])
-            nc.vector.tensor_copy(wsp[t][:], ws[:].rearrange("p (m t) -> p m t", t=PACK)[:, :, t])
+        def deal_weights(words, scales, pair):
+            planes = part(pair, 2)
+            nc.vector.tensor_copy(
+                words[:].bitcast(U16).rearrange("p (d c m) -> p c d m", d=2, m=4),
+                w_word_tile[:].bitcast(U16).rearrange("p (c m d) -> p c d m", m=4, d=PACK)[:, :, planes, :],
+            )
+            nc.vector.tensor_copy(
+                scales[:].rearrange("p (d c m) -> p c d m", d=2, m=8),
+                w_scale_tile[:].rearrange("p (c m d) -> p c d m", m=8, d=PACK)[:, :, planes, :],
+            )
+            return [(words[:, part(d, E * 2 * P)], scales[:, part(d, E * P)]) for d in range(2)]
 
-        ident = keep.tile([P, P], F32, name="ident")
-        make_identity(nc, ident[:])
-        ident_bf = keep.tile([P, P], BF16, name="ident_bf")
-        make_identity(nc, ident_bf[:])
-
-        H = T // 2
-        half = [slice(h * H, (h + 1) * H) for h in range(2)]
-        half_list = [slice(h * H // 16, (h + 1) * H // 16) for h in range(2)]
-
-        def bank(name, k, dtype=F32):
-            return psum.tile([P, 2 * C], dtype, name=name, offset=k * BANK)[:]
-
-        def six_banks(name):
-            return [bank(f"{name}_{k}", k) for k in range(2, 8)]
-
-        def multiply(dst, words, scales, e, t):
+        def multiply(sums, words, scales, e, d):
             nc.tensor.matmul_mx(
-                out=dst,
-                lhsT=wwp[t][:, e * 2 * P : (e + 1) * 2 * P].bitcast(FP4X4),
-                lhsT_scale=wsp[t][:, e * P : (e + 1) * P],
+                out=sums,
+                lhsT=dealt[d][0][:, part(e, 2 * P)].bitcast(FP4X4),
+                lhsT_scale=dealt[d][1][:, part(e, P)],
                 rhs=words.bitcast(FP8X4),
                 rhs_scale=scales,
                 start=True,
                 stop=True,
             )
 
-        def sum_turned(left, right, name, acc, dtype=F32):
-            blocks = [slice(j * P, (j + 1) * P) for j in range(T // P)]
-            for j, blk in enumerate(blocks):
-                nc.tensor.matmul(acc[:, blk], left[:, blk], ident[:], start=(j == 0), stop=False, is_transpose=True)
-            for j, blk in enumerate(blocks):
-                nc.tensor.matmul(acc[:, blk], right[:, blk], ident[:], start=False, stop=(j == len(blocks) - 1), is_transpose=True)
-            turned = keep.tile([P, T], dtype, name=f"turned{name}", tag=f"turned{name}", align_bytes=64)
-            nc.scalar.copy(turned[:], acc)
+        def fetch(terms, results, gate, d, tokens, columns):
+            for r, (term, pos) in enumerate(terms):
+                window = results[d][:].indirect(entries(pos, tokens.start, tokens.stop))
+                nc.vector.tensor_tensor(term[:, columns], window, gate[:, r, tokens], MULT)
+
+        def term_tiles(name, width, pos_a, pos_b):
+            return [(keep.tile([P, width], F32, name=f"{name}_{r}"), pos) for r, pos in enumerate((pos_a, pos_b))]
+
+        def sum_turned(terms, name, sums, dtype):
+            blocks = [(term, part(j, P)) for term, pos in terms for j in range(T // P)]
+            for n, (term, block) in enumerate(blocks):
+                nc.tensor.matmul(
+                    sums[:, block], term[:, block], identity[:], start=(n == 0), stop=(n == len(blocks) - 1), is_transpose=True
+                )
+            turned = keep.tile([P, T], dtype, name=name, tag=name, align_bytes=64)
+            nc.scalar.copy(turned[:], sums)
             return turned
 
-        def turn_back(turned, back, identity=ident):
+        def turn_back(turned, back, unit):
             for j in range(T // P):
-                blk = slice(j * P, (j + 1) * P)
-                nc.tensor.transpose(back[:, blk], turned[:, blk], identity[:])
+                nc.tensor.transpose(back[:, part(j, P)], turned[:, part(j, P)], unit[:])
             return back
 
-        def fetch(dst, src, pos, gate):
-            nc.vector.tensor_tensor(dst, src[:].indirect(pos), gate, MULT)
-
-        def fetch_all(src, pos_a, pos_b, gate, step, cuts, first_sum=None):
-            widths = [T, T] + [2 * (hi - lo) for lo, hi in cuts]
-            a = [keep.tile([P, w], F32, name=f"a{step}_{j}") for j, w in enumerate(widths)]
-            b = [keep.tile([P, w], F32, name=f"b{step}_{j}") for j, w in enumerate(widths)]
-            for t in range(2):
-                fetch(a[t][:], src[t], pos_a[:], gate[:, 0, :])
-                fetch(b[t][:], src[t], pos_b[:], gate[:, 1, :])
-            for h, (lo, hi) in enumerate(cuts):
-                w, entries, tokens = hi - lo, slice(lo // 16, hi // 16), slice(lo, hi)
-                for u in range(2):
-                    fetch(a[2 + h][:, u * w : (u + 1) * w], src[2 + u], pos_a[:, entries], gate[:, 0, tokens])
-                    if (h, u) == (1, 0):
-                        nc.vector.tensor_tensor(first_sum, a[2][:], b[2][:], ADD)
-                    fetch(b[2 + h][:, u * w : (u + 1) * w], src[2 + u], pos_b[:, entries], gate[:, 1, tokens])
-            return a, b
-
-        gw = keep.tile([P, S], U32, name="gw", align_bytes=64)
-        gs = [keep.tile([P, 2 * C], U8, name=f"gs{h}", align_bytes=64) for h in range(2)]
-        y = [keep.tile([P, S], F32, name=f"y{t}") for t in range(PACK)]
-        nc.vector.tensor_copy(gw[:], xw[:].bitcast(U32).indirect(offs_t[:]))
-        g1 = keep.tile([P, 2, T], F32, name="g1", tag="early", align_bytes=64)
-        nc.sync.dma_start(g1[:], gate1.rearrange("r p t -> p r t"))
-        deal_weights(0)
-        deal_weights(1)
+        slot_words = keep.tile([P, S], U32, name="slot_words", align_bytes=64)
+        slot_scales = [keep.tile([P, 2 * C], U8, name=f"slot_scales{h}", align_bytes=64) for h in range(2)]
+        y = [keep.tile([P, S], F32, name=f"y{d}") for d in range(PACK)]
+        nc.vector.tensor_copy(slot_words[:], x_window[:].bitcast(U32).indirect(offs_tile[:]))
+        gate1_tile = keep.tile([P, 2, T], F32, name="gate1_tile", tag="x_then_gate1", align_bytes=64)
+        nc.sync.dma_start(gate1_tile[:], gate1.rearrange("r p t -> p r t"))
+        dealt = deal_weights(
+            keep.tile([P, 2 * E * 2 * P], U8, name="dealt_words01", align_bytes=64),
+            keep.tile([P, 2 * E * P], U8, name="dealt_scales01", align_bytes=64),
+            0,
+        )
         for h in range(2):
-            nc.vector.tensor_copy(gs[h][:], xs[:, :S].indirect(offs_t[:, 2 * h * COLS : 2 * (h + 1) * COLS]))
-        deal_weights(2)
-        deal_weights(3)
-        g2 = keep.tile([P, 2, T], F32, name="g2", tag="late", align_bytes=64)
-        nc.sync.dma_start(g2[:], gate2.rearrange("r p t -> p r t"))
+            nc.vector.tensor_copy(slot_scales[h][:], x_scale_window.indirect(entries(offs_tile, 2 * h * C, 2 * (h + 1) * C)))
+        dealt = dealt + deal_weights(
+            reuse.tile([P, 2 * E * 2 * P], U8, name="dealt_words23", offset=0, align_bytes=64),
+            reuse.tile([P, 2 * E * P], U8, name="dealt_scales23", offset=2 * E * 2 * P, align_bytes=64),
+            1,
+        )
+        gate2_tile = keep.tile([P, 2, T], F32, name="gate2_tile", tag="w_then_gate2", align_bytes=64)
+        nc.sync.dma_start(gate2_tile[:], gate2.rearrange("r p t -> p r t"))
 
-        def first_step(acc, t, h):
+        def expert_pair(sums, d, h):
             for u in range(2):
-                e = 2 * h + u
-                multiply(acc[:, half[u]], gw[:, e * C : (e + 1) * C], gs[h][:, half[u]], e, t)
-            nc.scalar.activation(y[t][:, 2 * h * C : 2 * (h + 1) * C], acc, GELU)
+                multiply(sums[:, part(u, C)], slot_words[:, part(2 * h + u, C)], slot_scales[h][:, part(u, C)], 2 * h + u, d)
+            nc.scalar.activation(y[d][:, part(h, 2 * C)], sums, GELU)
 
-        first_step(bank("mm1_0", 0), 0, 0)
-        first_step(psum.tile([P, 2 * 2 * C], F32, name="mm1_1", offset=BANK)[:, : 2 * C], 0, 1)
-        banks = six_banks("mm1")
-        for t in range(1, PACK):
-            for h in range(2):
-                first_step(banks[2 * (t - 1) + 1 - h], t, 1 - h)
+        expert_pair(bank("y_0_0", 0), 0, 0)
+        expert_pair(bank("y_0_1", 1, span=2), 0, 1)
+        for d in range(1, PACK):
+            for h in (1, 0):
+                expert_pair(bank(f"y_{d}_{h}", 2 * d + h), d, h)
 
-        a, b = fetch_all(y, pos1_t, pos2_t, g1, 1, [(0, T)])
-        c_single = [keep.tile([P, T], BF16, name=f"c{t}", align_bytes=64) for t in range(2)]
-        c_pair_bf = c_pair[:, :T].bitcast(BF16)
-        both = [keep.tile([P, 2 * C], I32, name=f"both{e}", align_bytes=64) for e in range(2)]
+        everyone = slice(0, T)
+        low_terms = [term_tiles(f"c_terms{d}", T, pos1_tile, pos2_tile) for d in range(2)]
+        high_terms = term_tiles("c_terms_high", 2 * T, pos1_tile, pos2_tile)
+        for d in range(2):
+            fetch(low_terms[d], y, gate1_tile, d, everyone, everyone)
+        for u in range(2):
+            fetch(high_terms, y, gate1_tile, 2 + u, everyone, part(u, T))
 
-        def gather_single(dst_words, e, t):
-            dst = dst_words.bitcast(BF16).rearrange("p (c u) -> p c u", u=2)[:, :, t]
-            nc.scalar.activation(dst, c_single[t][:].indirect(offs2_t[:, e * COLS : (e + 1) * COLS]), COPY)
+        c_low = [keep.tile([P, T], BF16, name=f"c_low{d}", align_bytes=64) for d in range(2)]
+        halves = [keep.tile([P, 2 * C], I32, name=f"halves{e}", align_bytes=64) for e in range(2)]
 
-        turned = [sum_turned(a[t], b[t], f"1{t}", bank(f"acc1{t}", 2 * t), BF16) for t in range(2)]
-        nc.scalar.copy(c_single[0][:], turn_back(turned[0], bank("back10", 1, BF16), ident_bf))
-        gather_single(both[0][:, :C], 0, 0)
-        nc.scalar.copy(c_single[1][:], turn_back(turned[1], bank("back11", 3, BF16), ident_bf))
-        gather_single(both[1][:, :C], 1, 0)
-        gather_single(both[0][:, :C], 0, 1)
-        gather_single(both[1][:, :C], 1, 1)
-        both23 = keep.tile([P, 4 * C], I32, name="both23", tag="turned11", align_bytes=64)
+        def gather_low(words, e, d):
+            values = words.bitcast(BF16).rearrange("p (c u) -> p c u", u=2)[:, :, d]
+            nc.scalar.activation(values, c_low[d][:].indirect(entries(offs2_tile, e * C, (e + 1) * C)), COPY)
+
+        turned = [sum_turned(low_terms[d], f"c_turned{d}", bank(f"c_sums{d}", 2 * d), BF16) for d in range(2)]
+        nc.scalar.copy(c_low[0][:], turn_back(turned[0], bank("c_back0", 1, BF16), identity_bf16))
+        gather_low(halves[0][:, :C], 0, 0)
+        nc.scalar.copy(c_low[1][:], turn_back(turned[1], bank("c_back1", 3, BF16), identity_bf16))
+        gather_low(halves[1][:, :C], 1, 0)
+        for e in range(2):
+            gather_low(halves[e][:, :C], e, 1)
+        halves23 = keep.tile([P, 4 * C], I32, name="halves23", tag="c_turned1", align_bytes=64)
         for e in range(2, E):
-            for t in range(2):
-                gather_single(both23[:, (e - 2) * C : (e - 1) * C], e, t)
+            for d in range(2):
+                gather_low(halves23[:, part(e - 2, C)], e, d)
         nc.vector.tensor_tensor(
-            c_pair_bf.rearrange("p (c i u) -> p c u i", i=4, u=2),
-            a[2][:].rearrange("p (u c i) -> p c u i", u=2, i=4),
-            b[2][:].rearrange("p (u c i) -> p c u i", u=2, i=4),
+            c_pairs[:, :T].bitcast(BF16).rearrange("p (c i u) -> p c u i", i=RUN, u=2),
+            high_terms[0][0][:].rearrange("p (u c i) -> p c u i", u=2, i=RUN),
+            high_terms[1][0][:].rearrange("p (u c i) -> p c u i", u=2, i=RUN),
             ADD,
         )
 
-        groups = [(0, 1, both[0][:]), (2, 2, both23[:]), (1, 1, both[1][:])]
-        xq = [keep.tile([P, n * C * PACK], BF16, name=f"xq{e}", align_bytes=64) for e, n, src in groups]
-        qw = [keep.tile([P, n * C], U32, name=f"qw{e}", tag=f"qw{e}", align_bytes=64) for e, n, src in groups]
-        qs = [keep.tile([P, n * C], U8, name=f"qs{e}", tag=f"qs{e}", align_bytes=64) for e, n, src in groups]
+        def gather_high(tile, lo, hi):
+            window = c_pairs[:].bitcast(U32).indirect(entries(offs2_tile, lo, hi))
+            nc.vector.tensor_copy(tile[:, hi - lo :].bitcast(U32), window)
 
-        def gather_pair(g):
-            e, n, src = groups[g]
-            nc.vector.tensor_copy(src[:, n * C :].bitcast(U32), c_pair[:].bitcast(U32).indirect(offs2_t[:, e * COLS : (e + n) * COLS]))
+        def weave(copy, dtype, woven, tile):
+            copy(woven[:].bitcast(dtype).rearrange("p (c u) -> p c u", u=2), tile[:].bitcast(dtype).rearrange("p (u c) -> p c u", u=2))
 
-        def weave(g, copy):
-            dst = xq[g][:].bitcast(U32).rearrange("p (c u) -> p c u", u=2)
-            copy(dst, groups[g][2].bitcast(U32).rearrange("p (u c) -> p c u", u=2))
+        woven = [keep.tile([P, C * PACK], BF16, name=f"woven{e}", align_bytes=64) for e in range(2)]
+        woven23 = keep.tile([P, 2 * C * PACK], BF16, name="woven23", align_bytes=64)
+        for e in range(2):
+            gather_high(halves[e], e * C, (e + 1) * C)
+        gather_high(halves23, 2 * C, S)
+        for e in range(2):
+            weave(nc.scalar.copy, U32, woven[e], halves[e])
+        weave(nc.vector.tensor_copy, I32, woven23, halves23)
 
-        def quantise(g):
-            nc.vector.quantize_mx(out=qw[g][:].bitcast(FP8X4), scales=qs[g][:], in_=xq[g][:])
+        c_values = [woven[0][:], woven[1][:], woven23[:, part(0, C * PACK)], woven23[:, part(1, C * PACK)]]
+        c_words = [keep.tile([P, C], U32, name=f"c_words{e}", align_bytes=64) for e in range(E)]
+        c_scales = [keep.tile([P, C], U8, name=f"c_scales{e}", align_bytes=64) for e in range(E)]
+        order = (0, 2, 1, 3)
+        for e in order:
+            nc.vector.quantize_mx(out=c_words[e][:].bitcast(FP8X4), scales=c_scales[e][:], in_=c_values[e])
 
-        gather_pair(0)
-        gather_pair(2)
-        gather_pair(1)
-        weave(0, nc.scalar.copy)
-        weave(2, nc.scalar.copy)
-        dst = xq[1][:].bitcast(I32).rearrange("p (c u) -> p c u", u=2)
-        nc.vector.tensor_copy(dst, both23[:].rearrange("p (u c) -> p c u", u=2))
-        quantise(0)
-        quantise(1)
-        quantise(2)
-
-        z = [keep.tile([P, S], F32, name=f"z{t}", align_bytes=64) for t in range(PACK)]
-        operands = [(qw[0][:], qs[0][:]), (qw[2][:], qs[2][:]), (qw[1][:, half[0]], qs[1][:, half[0]]), (qw[1][:, half[1]], qs[1][:, half[1]])]
-        wide = psum.tile([P, 6 * 2 * C], F32, name="mm2_last", offset=2 * BANK)
-        banks = [bank("mm2_pair", 0), bank("mm2_third", 1), wide[:, : 2 * C]]
-        for g, (e0, n, src) in enumerate(groups):
-            for e in range(e0, e0 + n):
-                multiply(banks[g][:, half[e - e0]], *operands[e], e, 0)
-            nc.scalar.activation(z[0][:, e0 * C : (e0 + n) * C], banks[g][:, : n * C], GELU)
-        banks = six_banks("mm2_rest")
-        for t in range(1, PACK):
+        z = [keep.tile([P, S], F32, name=f"z{d}", align_bytes=64) for d in range(PACK)]
+        for n, e in enumerate(order):
+            sums = bank(f"z_0_{e}", n, span=(5 if n == E - 1 else 1))[:, :C]
+            multiply(sums, c_words[e][:], c_scales[e][:], e, 0)
+            nc.scalar.activation(z[0][:, part(e, C)], sums, GELU)
+        later = {(d, h): bank(f"z_{d}_{h}", 2 * d + h) for d in range(1, PACK) for h in range(2)}
+        for d in range(1, PACK):
             for e in range(E):
-                multiply(banks[2 * (t - 1) + e // 2][:, half[e % 2]], *operands[e], e, t)
-        for t in range(1, PACK):
+                multiply(later[d, e // 2][:, part(e % 2, C)], c_words[e][:], c_scales[e][:], e, d)
+        for d in range(1, PACK):
             for h in range(2):
-                nc.scalar.activation(z[t][:, 2 * h * C : 2 * (h + 1) * C], banks[2 * (t - 1) + h], GELU)
+                nc.scalar.activation(z[d][:, part(h, 2 * C)], later[d, h], GELU)
 
-        cuts = [(0, H), (H, H + P), (H + P, T)]
-        o_first = keep.tile([P, PACK * H], F32, name="o_first")
-        a2, b2 = fetch_all(z, pos3_t, pos4_t, g2, 2, cuts, o_first[:, 2 * H :])
-        o_second = keep.tile([P, PACK * H], F32, name="o_second")
-        oq = [keep.tile([P, H, PACK], BF16, name=f"oq{h}", align_bytes=64) for h in range(2)]
-        ow = [keep.tile([P, H], I32, name=f"ow{h}", align_bytes=64) for h in range(2)]
-        osc = keep.tile([P, T], U8, name="osc", align_bytes=64)
-        out_rows = out_0.rearrange("(p t) n -> p t n", t=PACK)
+        result = keep.tile([P, 2 * PACK * H], F32, name="result")
+        by_half = result[:].rearrange("p (h d n) -> p h d n", h=2, d=PACK)
+        quarters = [slice(H, H + P), slice(H + P, T)]
+        low_terms = [term_tiles(f"out_terms{d}", T, pos3_tile, pos4_tile) for d in range(2)]
+        half_terms = term_tiles("out_terms_half", 2 * H, pos3_tile, pos4_tile)
+        quarter_terms = [term_tiles(f"out_terms_quarter{j}", 2 * P, pos3_tile, pos4_tile) for j in range(2)]
+
+        def add_high(terms, planes):
+            left, right = [term[:].rearrange("p (u n) -> p u n", u=2) for term, pos in terms]
+            nc.vector.tensor_tensor(planes, left, right, ADD)
+
+        for d in range(2):
+            fetch(low_terms[d], z, gate2_tile, d, everyone, everyone)
+        for u in range(2):
+            fetch(half_terms, z, gate2_tile, 2 + u, part(0, H), part(u, H))
+        fetch(quarter_terms[0], z, gate2_tile, 2, quarters[0], part(0, P))
+        add_high(half_terms, by_half[:, 0, 2:4, :])
+        fetch(quarter_terms[0], z, gate2_tile, 3, quarters[0], part(1, P))
+        for u in range(2):
+            fetch(quarter_terms[1], z, gate2_tile, 2 + u, quarters[1], part(u, P))
+
+        out_planes = out_0.rearrange("(p d) n -> p d n", d=PACK)
         out_words = out_1[0].rearrange("p t d -> p (t d)").bitcast(I32)
+        out_scales = keep.tile([P, T], U8, name="out_scales", align_bytes=64)
 
-        def planes(h):
-            nc.vector.quantize_mx(out=ow[h][:].bitcast(FP8X4), scales=osc[:, half[h]], in_=oq[h][:].rearrange("p c t -> p (c t)"))
-            nc.sync.dma_start(out_words[:, half[h]], ow[h][:])
+        def round_planes(copy, values, planes):
+            copy(values.rearrange("p (c i d) -> p c d i", i=RUN, d=PACK), planes.rearrange("p d (c i) -> p c d i", i=RUN))
 
-        turned = [sum_turned(a2[t], b2[t], f"2{t}", bank(f"acc2{t}", 2 * t)) for t in range(2)]
-        for t in range(2):
-            back = turn_back(turned[t], bank(f"back2{t}", 2 * t + 1))
-            nc.scalar.copy(o_first[:, t * H : (t + 1) * H], back[:, half[0]])
-            nc.scalar.copy(o_second[:, t * H : (t + 1) * H], back[:, half[1]])
-        first = o_first[:].rearrange("p (t n) -> p t n", t=PACK)
-        second = o_second[:].rearrange("p (t n) -> p t n", t=PACK)
-        nc.scalar.dma_start(out_rows[:, 0:2, half[0]], first[:, 0:2, :])
-        nc.scalar.dma_start(out_rows[:, 0:2, half[1]], second[:, 0:2, :])
-        nc.sync.dma_start(out_rows[:, 2:4, half[0]], first[:, 2:4, :])
-        nc.scalar.copy(
-            oq[0][:].rearrange("p (c i) t -> p c t i", i=4), o_first[:].rearrange("p (t c i) -> p c t i", t=PACK, i=4)
-        )
+        def quantise_half(h):
+            words = keep.tile([P, H], I32, name=f"out_words{h}", align_bytes=64)
+            nc.vector.quantize_mx(out=words[:].bitcast(FP8X4), scales=out_scales[:, part(h, H)], in_=rounded[h][:])
+            nc.sync.dma_start(out_words[:, part(h, H)], words[:])
+
+        def store_low(d):
+            nc.scalar.dma_start(out_planes[:, d, :].rearrange("p (h n) -> p h n", h=2), by_half[:, :, d, :])
+
+        turned = [sum_turned(low_terms[d], f"out_turned{d}", bank(f"out_sums{d}", 2 * d), F32) for d in range(2)]
+        for d in range(2):
+            back = turn_back(turned[d], bank(f"out_back{d}", 2 * d + 1), identity)
+            nc.scalar.copy(by_half[:, :, d, :], back.rearrange("p (h n) -> p h n", h=2))
+        store_low(0)
+        nc.sync.dma_start(out_planes[:, 2:4, part(0, H)], by_half[:, 0, 2:4, :])
+        rounded = [keep.tile([P, H * PACK], BF16, name=f"rounded{h}", align_bytes=64) for h in range(2)]
+        round_planes(nc.scalar.copy, rounded[0][:], by_half[:, 0, :, :])
+        store_low(1)
         for j in range(2):
-            nc.vector.tensor_tensor(
-                second[:, 2:4, j * P : (j + 1) * P],
-                a2[3 + j][:].rearrange("p (u t) -> p u t", u=2),
-                b2[3 + j][:].rearrange("p (u t) -> p u t", u=2),
-                ADD,
-            )
-        nc.sync.dma_start(out_rows[:, 2:4, half[1]], second[:, 2:4, :])
+            add_high(quarter_terms[j], by_half[:, 1, 2:4, part(j, P)])
+        nc.sync.dma_start(out_planes[:, 2:4, part(1, H)], by_half[:, 1, 2:4, :])
         for j in range(2):
-            tokens = slice(j * P, (j + 1) * P)
-            nc.vector.tensor_copy(
-                oq[1][:, tokens, :].rearrange("p (c i) t -> p c t i", i=4), second[:, :, tokens].rearrange("p t (c i) -> p c t i", i=4)
-            )
-        planes(0)
-        planes(1)
-        out_s = out_2[0].bitcast(I32)
+            round_planes(nc.vector.tensor_copy, rounded[1][:, part(j, P * PACK)], by_half[:, 1, :, part(j, P)])
+        for h in range(2):
+            quantise_half(h)
+
+        scale_rows = out_2[0].bitcast(I32)
         for q in range(4):
             queue = nc.sync if q % 2 else nc.scalar
-            queue.dma_start(out_s[4 * q : 4 * q + 4, :], osc[32 * q : 32 * q + 4, :].bitcast(I32))
+            queue.dma_start(scale_rows[part(q, 4), :], out_scales[32 * q : 32 * q + 4, :].bitcast(I32))

from contextlib import ExitStack

import concourse.mybir as mybir
from concourse.masks import make_identity

K, T, E, C = 512, 512, 4, 256
S = E * C
P = 128
PACK = 4
H = T // 2
ENTRIES = 16
BANK = 2048
RUN = 4
FLOPS = 2 * 2 * K * K * S

F32 = mybir.dt.float32
BF16 = mybir.dt.bfloat16
I32 = mybir.dt.int32
U32 = mybir.dt.uint32
U16 = mybir.dt.uint16
U8 = mybir.dt.uint8
FP8X4 = mybir.dt.float8_e4m3fn_x4
FP4X4 = mybir.dt.float4_e2m1fn_x4
MULT = mybir.AluOpType.mult
ADD = mybir.AluOpType.add
GELU = mybir.ActivationFunctionType.Gelu_apprx_tanh
COPY = mybir.ActivationFunctionType.Copy


def part(index, width):
    return slice(index * width, (index + 1) * width)


def entries(offsets, lo, hi):
    return offsets[:, lo // ENTRIES : hi // ENTRIES]


def tile_moe_uni_gelu_kernel(
    tc, x_words, x_scales, w_words, w_scales, gate1, gate2, offs, pos1, pos2, offs2, pos3, pos4, out_0, out_1, out_2
):
    nc = tc.nc
    with ExitStack() as ctx:
        lists = ctx.enter_context(tc.tile_pool(name="lists", bufs=1))
        keep = ctx.enter_context(tc.tile_pool(name="keep", bufs=1))
        reuse = ctx.enter_context(tc.tile_pool(name="reuse", bufs=1))
        psum = ctx.enter_context(tc.psum_pool(name="psum", bufs=1))

        def load_list(name, source):
            tile = lists.tile(list(source.shape), U16, name=name)
            nc.sync.dma_start(tile[:], source)
            return tile

        def bank(name, first, dtype=F32, span=1):
            return psum.tile([P, span * 2 * C], dtype, name=name, offset=first * BANK)[:, : 2 * C]

        x_scale_tile = reuse.tile([P, 3 * S], U8, name="x_scale_tile", offset=0, align_bytes=64)
        x_scale_window = x_scale_tile[:, : 2 * T]
        x_window = keep.tile([P, 2 * S], I32, name="x_window", tag="x_then_gate1", align_bytes=64)
        w_scale_tile = keep.tile([P, E * K], U8, name="w_scale_tile", align_bytes=64)
        nc.vector.memset(w_scale_tile[:].bitcast(I32), 0)
        nc.gpsimd.memset(x_scale_window.bitcast(I32), 0)
        nc.vector.memset(x_window[:, T:], 0)
        c_pairs = keep.tile([P, 2 * T], I32, name="c_pairs", align_bytes=64)
        nc.vector.memset(c_pairs[:, T:], 0)

        offs_tile = load_list("offs_tile", offs)
        nc.sync.dma_start(x_window[:, :T], x_words[0].rearrange("p t d -> p (t d)").bitcast(I32))
        w_word_tile = keep.tile([P, E * 2 * K], U8, name="w_word_tile", tag="w_then_gate2", align_bytes=64)
        nc.sync.dma_start(
            w_word_tile[:].bitcast(I32).rearrange("p (e n) -> p e n", e=E),
            w_words.rearrange("e s p n -> p (e s) n").bitcast(I32),
        )
        w_scale_rows = w_scales.bitcast(I32).rearrange("e s (q r) n -> r q (e s) n", r=4)
        for r in range(4):
            nc.sync.dma_start(w_scale_tile[r:P:32, :].bitcast(I32).rearrange("q (e n) -> q e n", e=E), w_scale_rows[r])
        x_scale_rows = x_scales[0].bitcast(I32).rearrange("(q r) n -> r q n", r=4)
        for r in range(4):
            nc.sync.dma_start(x_scale_tile[r:P:32, :T].bitcast(I32), x_scale_rows[r])
        pos1_tile = load_list("pos1_tile", pos1)
        pos2_tile = load_list("pos2_tile", pos2)
        offs2_tile = load_list("offs2_tile", offs2)
        pos3_tile = load_list("pos3_tile", pos3)
        pos4_tile = load_list("pos4_tile", pos4)

        identity = keep.tile([P, P], F32, name="identity")
        make_identity(nc, identity[:])
        identity_bf16 = keep.tile([P, P], BF16, name="identity_bf16")
        make_identity(nc, identity_bf16[:])

        def deal_weights(words, scales, pair):
            planes = part(pair, 2)
            nc.vector.tensor_copy(
                words[:].bitcast(U16).rearrange("p (d c m) -> p c d m", d=2, m=4),
                w_word_tile[:].bitcast(U16).rearrange("p (c m d) -> p c d m", m=4, d=PACK)[:, :, planes, :],
            )
            nc.vector.tensor_copy(
                scales[:].rearrange("p (d c m) -> p c d m", d=2, m=8),
                w_scale_tile[:].rearrange("p (c m d) -> p c d m", m=8, d=PACK)[:, :, planes, :],
            )
            return [(words[:, part(d, E * 2 * P)], scales[:, part(d, E * P)]) for d in range(2)]

        def multiply(sums, words, scales, e, d):
            nc.tensor.matmul_mx(
                out=sums,
                lhsT=dealt[d][0][:, part(e, 2 * P)].bitcast(FP4X4),
                lhsT_scale=dealt[d][1][:, part(e, P)],
                rhs=words.bitcast(FP8X4),
                rhs_scale=scales,
                start=True,
                stop=True,
            )

        def fetch(terms, results, gate, d, tokens, columns):
            for r, (term, pos) in enumerate(terms):
                window = results[d][:].indirect(entries(pos, tokens.start, tokens.stop))
                nc.vector.tensor_tensor(term[:, columns], window, gate[:, r, tokens], MULT)

        def term_tiles(name, width, pos_a, pos_b):
            return [(keep.tile([P, width], F32, name=f"{name}_{r}"), pos) for r, pos in enumerate((pos_a, pos_b))]

        def sum_turned(terms, name, sums, dtype):
            blocks = [(term, part(j, P)) for term, pos in terms for j in range(T // P)]
            for n, (term, block) in enumerate(blocks):
                nc.tensor.matmul(
                    sums[:, block], term[:, block], identity[:], start=(n == 0), stop=(n == len(blocks) - 1), is_transpose=True
                )
            turned = keep.tile([P, T], dtype, name=name, tag=name, align_bytes=64)
            nc.scalar.copy(turned[:], sums)
            return turned

        def turn_back(turned, back, unit):
            for j in range(T // P):
                nc.tensor.transpose(back[:, part(j, P)], turned[:, part(j, P)], unit[:])
            return back

        slot_words = keep.tile([P, S], U32, name="slot_words", align_bytes=64)
        slot_scales = [keep.tile([P, 2 * C], U8, name=f"slot_scales{h}", align_bytes=64) for h in range(2)]
        y = [keep.tile([P, S], F32, name=f"y{d}") for d in range(PACK)]
        nc.vector.tensor_copy(slot_words[:], x_window[:].bitcast(U32).indirect(offs_tile[:]))
        gate1_tile = keep.tile([P, 2, T], F32, name="gate1_tile", tag="x_then_gate1", align_bytes=64)
        nc.sync.dma_start(gate1_tile[:], gate1.rearrange("r p t -> p r t"))
        dealt = deal_weights(
            keep.tile([P, 2 * E * 2 * P], U8, name="dealt_words01", align_bytes=64),
            keep.tile([P, 2 * E * P], U8, name="dealt_scales01", align_bytes=64),
            0,
        )
        for h in range(2):
            nc.vector.tensor_copy(slot_scales[h][:], x_scale_window.indirect(entries(offs_tile, 2 * h * C, 2 * (h + 1) * C)))
        dealt = dealt + deal_weights(
            reuse.tile([P, 2 * E * 2 * P], U8, name="dealt_words23", offset=0, align_bytes=64),
            reuse.tile([P, 2 * E * P], U8, name="dealt_scales23", offset=2 * E * 2 * P, align_bytes=64),
            1,
        )
        gate2_tile = keep.tile([P, 2, T], F32, name="gate2_tile", tag="w_then_gate2", align_bytes=64)
        nc.sync.dma_start(gate2_tile[:], gate2.rearrange("r p t -> p r t"))

        def expert_pair(sums, d, h):
            for u in range(2):
                multiply(sums[:, part(u, C)], slot_words[:, part(2 * h + u, C)], slot_scales[h][:, part(u, C)], 2 * h + u, d)
            nc.scalar.activation(y[d][:, part(h, 2 * C)], sums, GELU)

        expert_pair(bank("y_0_0", 0), 0, 0)
        expert_pair(bank("y_0_1", 1, span=2), 0, 1)
        for d in range(1, PACK):
            for h in (1, 0):
                expert_pair(bank(f"y_{d}_{h}", 2 * d + h), d, h)

        everyone = slice(0, T)
        low_terms = [term_tiles(f"c_terms{d}", T, pos1_tile, pos2_tile) for d in range(2)]
        high_terms = term_tiles("c_terms_high", 2 * T, pos1_tile, pos2_tile)
        for d in range(2):
            fetch(low_terms[d], y, gate1_tile, d, everyone, everyone)
        for u in range(2):
            fetch(high_terms, y, gate1_tile, 2 + u, everyone, part(u, T))

        c_low = [keep.tile([P, T], BF16, name=f"c_low{d}", align_bytes=64) for d in range(2)]
        halves = [keep.tile([P, 2 * C], I32, name=f"halves{e}", align_bytes=64) for e in range(2)]

        def gather_low(words, e, d):
            values = words.bitcast(BF16).rearrange("p (c u) -> p c u", u=2)[:, :, d]
            nc.scalar.activation(values, c_low[d][:].indirect(entries(offs2_tile, e * C, (e + 1) * C)), COPY)

        turned = [sum_turned(low_terms[d], f"c_turned{d}", bank(f"c_sums{d}", 2 * d), BF16) for d in range(2)]
        nc.scalar.copy(c_low[0][:], turn_back(turned[0], bank("c_back0", 1, BF16), identity_bf16))
        gather_low(halves[0][:, :C], 0, 0)
        nc.scalar.copy(c_low[1][:], turn_back(turned[1], bank("c_back1", 3, BF16), identity_bf16))
        gather_low(halves[1][:, :C], 1, 0)
        for e in range(2):
            gather_low(halves[e][:, :C], e, 1)
        halves23 = keep.tile([P, 4 * C], I32, name="halves23", tag="c_turned1", align_bytes=64)
        for e in range(2, E):
            for d in range(2):
                gather_low(halves23[:, part(e - 2, C)], e, d)
        nc.vector.tensor_tensor(
            c_pairs[:, :T].bitcast(BF16).rearrange("p (c i u) -> p c u i", i=RUN, u=2),
            high_terms[0][0][:].rearrange("p (u c i) -> p c u i", u=2, i=RUN),
            high_terms[1][0][:].rearrange("p (u c i) -> p c u i", u=2, i=RUN),
            ADD,
        )

        def gather_high(tile, lo, hi):
            window = c_pairs[:].bitcast(U32).indirect(entries(offs2_tile, lo, hi))
            nc.vector.tensor_copy(tile[:, hi - lo :].bitcast(U32), window)

        def weave(copy, dtype, woven, tile):
            copy(woven[:].bitcast(dtype).rearrange("p (c u) -> p c u", u=2), tile[:].bitcast(dtype).rearrange("p (u c) -> p c u", u=2))

        woven = [keep.tile([P, C * PACK], BF16, name=f"woven{e}", align_bytes=64) for e in range(2)]
        woven23 = keep.tile([P, 2 * C * PACK], BF16, name="woven23", align_bytes=64)
        for e in range(2):
            gather_high(halves[e], e * C, (e + 1) * C)
        gather_high(halves23, 2 * C, S)
        for e in range(2):
            weave(nc.scalar.copy, U32, woven[e], halves[e])
        weave(nc.vector.tensor_copy, I32, woven23, halves23)

        c_values = [woven[0][:], woven[1][:], woven23[:, part(0, C * PACK)], woven23[:, part(1, C * PACK)]]
        c_words = [keep.tile([P, C], U32, name=f"c_words{e}", align_bytes=64) for e in range(E)]
        c_scales = [keep.tile([P, C], U8, name=f"c_scales{e}", align_bytes=64) for e in range(E)]
        order = (0, 2, 1, 3)
        for e in order:
            nc.vector.quantize_mx(out=c_words[e][:].bitcast(FP8X4), scales=c_scales[e][:], in_=c_values[e])

        z = [keep.tile([P, S], F32, name=f"z{d}", align_bytes=64) for d in range(PACK)]
        for n, e in enumerate(order):
            sums = bank(f"z_0_{e}", n, span=(5 if n == E - 1 else 1))[:, :C]
            multiply(sums, c_words[e][:], c_scales[e][:], e, 0)
            nc.scalar.activation(z[0][:, part(e, C)], sums, GELU)
        later = {(d, h): bank(f"z_{d}_{h}", 2 * d + h) for d in range(1, PACK) for h in range(2)}
        for d in range(1, PACK):
            for e in range(E):
                multiply(later[d, e // 2][:, part(e % 2, C)], c_words[e][:], c_scales[e][:], e, d)
        for d in range(1, PACK):
            for h in range(2):
                nc.scalar.activation(z[d][:, part(h, 2 * C)], later[d, h], GELU)

        result = keep.tile([P, 2 * PACK * H], F32, name="result")
        by_half = result[:].rearrange("p (h d n) -> p h d n", h=2, d=PACK)
        quarters = [slice(H, H + P), slice(H + P, T)]
        low_terms = [term_tiles(f"out_terms{d}", T, pos3_tile, pos4_tile) for d in range(2)]
        half_terms = term_tiles("out_terms_half", 2 * H, pos3_tile, pos4_tile)
        quarter_terms = [term_tiles(f"out_terms_quarter{j}", 2 * P, pos3_tile, pos4_tile) for j in range(2)]

        def add_high(terms, planes):
            left, right = [term[:].rearrange("p (u n) -> p u n", u=2) for term, pos in terms]
            nc.vector.tensor_tensor(planes, left, right, ADD)

        for d in range(2):
            fetch(low_terms[d], z, gate2_tile, d, everyone, everyone)
        for u in range(2):
            fetch(half_terms, z, gate2_tile, 2 + u, part(0, H), part(u, H))
        fetch(quarter_terms[0], z, gate2_tile, 2, quarters[0], part(0, P))
        add_high(half_terms, by_half[:, 0, 2:4, :])
        fetch(quarter_terms[0], z, gate2_tile, 3, quarters[0], part(1, P))
        for u in range(2):
            fetch(quarter_terms[1], z, gate2_tile, 2 + u, quarters[1], part(u, P))

        out_planes = out_0.rearrange("(p d) n -> p d n", d=PACK)
        out_words = out_1[0].rearrange("p t d -> p (t d)").bitcast(I32)
        out_scales = keep.tile([P, T], U8, name="out_scales", align_bytes=64)

        def round_planes(copy, values, planes):
            copy(values.rearrange("p (c i d) -> p c d i", i=RUN, d=PACK), planes.rearrange("p d (c i) -> p c d i", i=RUN))

        def quantise_half(h):
            words = keep.tile([P, H], I32, name=f"out_words{h}", align_bytes=64)
            nc.vector.quantize_mx(out=words[:].bitcast(FP8X4), scales=out_scales[:, part(h, H)], in_=rounded[h][:])
            nc.sync.dma_start(out_words[:, part(h, H)], words[:])

        def store_low(d):
            nc.scalar.dma_start(out_planes[:, d, :].rearrange("p (h n) -> p h n", h=2), by_half[:, :, d, :])

        turned = [sum_turned(low_terms[d], f"out_turned{d}", bank(f"out_sums{d}", 2 * d), F32) for d in range(2)]
        for d in range(2):
            back = turn_back(turned[d], bank(f"out_back{d}", 2 * d + 1), identity)
            nc.scalar.copy(by_half[:, :, d, :], back.rearrange("p (h n) -> p h n", h=2))
        store_low(0)
        nc.sync.dma_start(out_planes[:, 2:4, part(0, H)], by_half[:, 0, 2:4, :])
        rounded = [keep.tile([P, H * PACK], BF16, name=f"rounded{h}", align_bytes=64) for h in range(2)]
        round_planes(nc.scalar.copy, rounded[0][:], by_half[:, 0, :, :])
        store_low(1)
        for j in range(2):
            add_high(quarter_terms[j], by_half[:, 1, 2:4, part(j, P)])
        nc.sync.dma_start(out_planes[:, 2:4, part(1, H)], by_half[:, 1, 2:4, :])
        for j in range(2):
            round_planes(nc.vector.tensor_copy, rounded[1][:, part(j, P * PACK)], by_half[:, 1, :, part(j, P)])
        for h in range(2):
            quantise_half(h)

        scale_rows = out_2[0].bitcast(I32)
        for q in range(4):
            queue = nc.sync if q % 2 else nc.scalar
            queue.dma_start(scale_rows[part(q, 4), :], out_scales[32 * q : 32 * q + 4, :].bitcast(I32))
